import numpy as np
import ml_dtypes


def mxq(x, axis, fmt="e4m3"):
    dtype, down = {"e4m3": (ml_dtypes.float8_e4m3fn, 7), "e5m2": (ml_dtypes.float8_e5m2, 14)}[fmt]
    v = np.moveaxis(np.asarray(x, np.float32).astype(ml_dtypes.bfloat16).astype(np.float64), axis, -1)
    blocks = v.reshape(v.shape[:-1] + (-1, 32))
    amax = np.abs(blocks).max(-1, keepdims=True)
    byte = np.maximum(np.where(amax > 0, np.frexp(amax)[1] - 1 + 127, 0) - down, 1)
    scale = np.exp2(byte - 127.0)
    codes = (blocks / scale).astype(np.float32).astype(dtype).astype(np.float64)
    return np.moveaxis((codes * scale).reshape(v.shape), -1, axis)


WIDE = False


def mx_kscale(k):
    if not WIDE:
        return np.ones(k)
    levels = np.array([10, -10, 5, -5, 0])
    if k % 512:
        return np.exp2(np.random.permutation(np.resize(levels, k // 32))).repeat(32)
    a = np.empty((k // 512, 16))
    for p in range(k // 512):
        a[p, :8] = np.random.permutation(np.resize(levels, 8))
        for g in range(8):
            far = levels[np.abs(levels - a[p, g]) >= 10]
            a[p, g + 8] = far[np.random.randint(len(far))]
    return np.exp2(a.ravel()).repeat(32)


def f64(x):
    return np.asarray(x).astype(np.float64)


def striped(idx):
    return np.tile(idx.reshape(-1, 16).T, (8, 1)).astype(np.uint16)


def unstriped(offs):
    return offs[:16].T.reshape(-1).astype(np.int64)


E2M1 = np.array([0.0, 0.5, 1.0, 1.5, 2.0, 3.0, 4.0, 6.0, -0.0, -0.5, -1.0, -1.5, -2.0, -3.0, -4.0, -6.0])


def pack_fp4(w):
    k, n = w.shape
    w = f64(np.asarray(w, np.float32).astype(ml_dtypes.bfloat16)).reshape(k // 32, 32, n)
    amax = np.abs(w).max(1)
    mant, ex = np.frexp(amax / 6.0)
    byte = np.clip(np.where(amax > 0, np.where(mant > 0.5, ex, ex - 1) + 127, 1), 1, 254)
    scaled = (w * np.exp2(127.0 - byte)[:, None, :]).reshape(k, n).astype(np.float32)
    c = np.ascontiguousarray(scaled.reshape(k // 512, 128, 4, n).transpose(0, 1, 3, 2)).astype(ml_dtypes.float4_e2m1fn).view(np.uint8) & 0xF
    words = (c[..., 0::2] | (c[..., 1::2] << 4)).reshape(k // 512, 128, 2 * n)
    return np.ascontiguousarray(words), np.ascontiguousarray(byte.astype(np.uint8).reshape(k // 512, 16, n))


def unpack_fp4(words, scales):
    g, _, n = scales.shape
    words = np.ascontiguousarray(words).reshape(g, 128, n, 2)
    nib = np.empty((g, 128, n, 4), np.uint8)
    nib[..., 0::2] = words & 0xF
    nib[..., 1::2] = words >> 4
    vals = E2M1[nib] * np.repeat(np.exp2(scales.astype(np.float64) - 127.0), 8, axis=1)[..., None]
    return vals.transpose(0, 1, 3, 2).reshape(g * 512, n)


def relu(v):
    return np.maximum(v, 0.0)


K, T, S, H, N, U = 512, 2048, 1024, 512, 128, 1024


def setup_inputs():
    n = np.random.standard_normal
    s = mx_kscale(K)[:, None]
    u = mx_kscale(H)
    packed_w3 = pack_fp4(n((H, N)) / np.sqrt(H) / u[:, None])
    return {
        "xT": (n((K, T)) * s).astype(np.float32),
        "w1": (n((K, H)) / np.sqrt(2 * K) / s * u).astype(np.float32),
        "w2": (n((K, H)) / np.sqrt(2 * K) / s * u).astype(np.float32),
        "w3_words": packed_w3[0],
        "w3_scales": packed_w3[1],
        "offs": striped(np.random.permutation(T)[:S]),
        "src": striped(np.random.permutation(S)[(S * np.random.uniform(0, 1, U) ** 4).astype(np.int64)]),
        "dst": striped(np.random.permutation(S)),
    }


def reference(xT, w1, w2, w3_words, w3_scales, offs, src, dst):
    xq = mxq(f64(xT)[:, unstriped(offs)], 0, "e4m3")
    y = mxq(f64(w1), 0, "e4m3").T @ xq
    e = mxq(f64(w2), 0, "e4m3").T @ xq
    z = relu(y[:, unstriped(src)] + e[:, unstriped(dst)])
    return unpack_fp4(w3_words, w3_scales).T @ mxq(z, 0, "e4m3")

@@ -1,0 +1,196 @@
+from contextlib import ExitStack
+
+import concourse.mybir as mybir
+
+K, T, S, H, N = 512, 2048, 1024, 512, 128
+FLOPS = 2 * K * H * S * 2 + 2 * H * N * S
+
+F32 = mybir.dt.float32
+BF16 = mybir.dt.bfloat16
+I32 = mybir.dt.int32
+U32 = mybir.dt.uint32
+U16 = mybir.dt.uint16
+U8 = mybir.dt.uint8
+FP8X4 = mybir.dt.float8_e4m3fn_x4
+FP4X4 = mybir.dt.float4_e2m1fn_x4
+ACT = mybir.ActivationFunctionType
+ADD = mybir.AluOpType.add
+
+P = 128
+HALF = 512
+X_CHUNKS = ((0, 0, 1024, 640), (0, 1024, 1024, 640), (1, 0, 512, 0), (1, 512, 512, 0), (1, 1024, 512, 0), (1, 1536, 512, 320))
+EDGE_CHUNKS = ((0, 256), (256, 256), (512, 256), (768, 128), (896, 128))
+
+
+def tile_picked_hub_relu_e_kernel(tc, xT, w1, w2, w3_words, w3_scales, offs, src, dst, out):
+    nc = tc.nc
+    with ExitStack() as ctx:
+        keep = ctx.enter_context(tc.tile_pool(name="keep", bufs=1))
+        psum = ctx.enter_context(tc.psum_pool(name="psum", bufs=1))
+
+        offs_sb = keep.tile([P, S // 16], U16, name="offs_sb")
+        src_sb = keep.tile([P, S // 16], U16, name="src_sb")
+        dst_sb = keep.tile([P, S // 16], U16, name="dst_sb")
+
+        w3_bytes = keep.tile([P, N], U8, name="w3_bytes", align_bytes=64)
+        w3_codes = keep.tile([P, 2 * N], U8, name="w3_codes", align_bytes=64)
+        nc.vector.memset(w3_bytes[:].bitcast(I32), 0)
+
+        x_rows = xT.rearrange("(p u e) t -> p u e t", u=2, e=2)
+        x_raw = []
+        for i, (u, c0, width, vec) in enumerate(X_CHUNKS):
+            raw = keep.tile([P, 2, width], F32, name=f"x_raw{i}")
+            nc.sync.dma_start(out=raw[:], in_=x_rows[:, u, :, c0 : c0 + width])
+            x_raw.append(raw)
+            if i == 1:
+                nc.sync.dma_start(offs_sb[:], offs)
+
+        def load_w(w, name):
+            rows = w.rearrange("(p j) c -> p j c", j=4)
+            parts = []
+            for half in range(2):
+                raw = keep.tile([P, 4, H // 2], F32, name=f"{name}_raw{half}", tag=f"{name}_raw{half}")
+                nc.sync.dma_start(out=raw[:], in_=rows[:, :, half * (H // 2) : (half + 1) * (H // 2)])
+                parts.append(raw)
+            return parts
+
+        w2_raw = load_w(w2, "w2")
+        w1_raw = load_w(w1, "w1")
+        nc.sync.dma_start(dst_sb[:], dst)
+        nc.sync.dma_start(src_sb[:], src)
+        nc.sync.dma_start(out=w3_codes[:].bitcast(I32), in_=w3_words[0].bitcast(I32))
+        for q in range(4):
+            nc.sync.dma_start(
+                out=w3_bytes[32 * q : 32 * q + 4, :].bitcast(I32),
+                in_=w3_scales[0, 4 * q : 4 * q + 4, :].bitcast(I32),
+            )
+
+        x_pairs = [keep.tile([P, 2 * T], BF16, name=f"x_pairs{u}") for u in range(2)]
+        x_picked = [keep.tile([P, 4 * HALF], BF16, name=f"x_picked{h}", align_bytes=64) for h in range(2)]
+
+        def cast_x(i):
+            u, c0, width, vec = X_CHUNKS[i]
+            pairs = x_pairs[u][:].rearrange("p (t e) -> p t e", e=2)
+            raw = x_raw[i][:].rearrange("p e t -> p t e")
+            nc.scalar.activation(out=pairs[:, c0 + vec : c0 + width, :], in_=raw[:, vec:width, :], func=ACT.Copy)
+            if vec:
+                nc.vector.tensor_copy(out=pairs[:, c0 : c0 + vec, :], in_=raw[:, 0:vec, :])
+
+        def gather_x(u, h):
+            words = x_picked[h][:].bitcast(U32).rearrange("p (n u) -> p n u", u=2)
+            cols = slice(h * HALF // 16, (h + 1) * HALF // 16)
+            nc.vector.tensor_copy(out=words[:, :, u], in_=x_pairs[u][:].bitcast(U32).indirect(offs_sb[:, cols]))
+
+        def quantize(values, width, name, tag=None):
+            codes = keep.tile([P, width], U32, name=f"{name}_codes", tag=tag or f"{name}_codes", align_bytes=64)
+            scales = keep.tile([P, width], U8, name=f"{name}_scales", align_bytes=64)
+            nc.vector.quantize_mx(out=codes[:].bitcast(FP8X4), scales=scales[:], in_=values)
+            return codes, scales
+
+        def weave_w(parts, name):
+            grouped = keep.tile([P, 4 * H], BF16, name=f"{name}_grouped", tag=f"{name}_grouped", align_bytes=64)
+            view = grouped[:].rearrange("p (t m j) -> p m j t", t=4, j=4)
+            for half in range(2):
+                nc.scalar.copy(
+                    out=view[:, half * 64 : (half + 1) * 64],
+                    in_=parts[half][:].rearrange("p j (m t) -> p m j t", t=4),
+                )
+            return grouped
+
+        cast_x(0)
+        cast_x(1)
+        gather_x(0, 0)
+        gather_x(0, 1)
+        for i in range(2, len(X_CHUNKS)):
+            cast_x(i)
+        w2_grouped = weave_w(w2_raw, "w2")
+        gather_x(1, 0)
+        gather_x(1, 1)
+        x_q = [quantize(x_picked[0][:], HALF, "x0")]
+        w2_q = quantize(w2_grouped[:], H, "w2")
+        x_q.append(quantize(x_picked[1][:], HALF, "x1", tag="w2_grouped"))
+        w1_grouped = weave_w(w1_raw, "w1")
+
+        def product(w_q, t, name, first=False):
+            rows = keep.tile([P, S], F32, name=f"{name}{t}")
+            cols = slice(t * P, (t + 1) * P)
+            for h in range(2):
+                bank = psum.tile([P, HALF], F32, name="bank", tag="bank", bufs=6)
+                nc.tensor.matmul_mx(
+                    out=bank[:],
+                    lhsT=w_q[0][:, cols].bitcast(FP8X4),
+                    lhsT_scale=w_q[1][:, cols],
+                    rhs=x_q[h][0][:].bitcast(FP8X4),
+                    rhs_scale=x_q[h][1][:],
+                    start=True,
+                    stop=True,
+                )
+                if first and h == 0:
+                    nc.vector.tensor_copy(out=rows[:, h * HALF : (h + 1) * HALF], in_=bank[:])
+                else:
+                    nc.scalar.copy(out=rows[:, h * HALF : (h + 1) * HALF], in_=bank[:])
+            return rows
+
+        e_picked = [keep.tile([P, S], F32, name=f"e_picked{t}") for t in range(4)]
+        sums = keep.tile([P, 4, S], F32, name="sums")
+
+        def gather_e(rows, t, r0, width):
+            cols = slice(r0 // 16, (r0 + width) // 16)
+            nc.vector.tensor_copy(out=e_picked[t][:, r0 : r0 + width], in_=rows[:].indirect(dst_sb[:, cols]))
+
+        def gather_y(rows, t, r0, width):
+            cols = slice(r0 // 16, (r0 + width) // 16)
+            nc.vector.tensor_tensor(
+                out=sums[:, t, r0 : r0 + width], in0=rows[:].indirect(src_sb[:, cols]), in1=e_picked[t][:, r0 : r0 + width], op=ADD
+            )
+
+        def relu(c):
+            r0, width = EDGE_CHUNKS[c]
+            z = keep.tile([P, 4 * width], BF16, name=f"z{c}", align_bytes=64)
+            nc.scalar.activation(
+                out=z[:].rearrange("p (n i t) -> p n t i", i=4, t=4),
+                in_=sums[:, :, r0 : r0 + width].rearrange("p t (n i) -> p n t i", i=4),
+                func=ACT.Relu,
+            )
+            return z
+
+        def finish(c, z):
+            r0, width = EDGE_CHUNKS[c]
+            codes, scales = quantize(z[:], width, f"z{c}")
+            bank = psum.tile([P, width], F32, name="out_bank", tag="out_bank", bufs=2)
+            nc.tensor.matmul_mx(
+                out=bank[:],
+                lhsT=w3_codes[:].bitcast(FP4X4),
+                lhsT_scale=w3_bytes[:],
+                rhs=codes[:].bitcast(FP8X4),
+                rhs_scale=scales[:],
+                start=True,
+                stop=True,
+            )
+            result = keep.tile([P, width], F32, name=f"result{c}")
+            if c == len(EDGE_CHUNKS) - 1:
+                nc.vector.tensor_copy(out=result[:], in_=bank[:])
+            else:
+                nc.scalar.copy(out=result[:], in_=bank[:])
+            nc.sync.dma_start(out=out[:, r0 : r0 + width], in_=result[:])
+
+        e_rows = [product(w2_q, 0, "e", first=True)]
+        w1_q = quantize(w1_grouped[:], H, "w1")
+        e_rows += [product(w2_q, 1, "e"), product(w2_q, 2, "e")]
+        y_rows = [product(w1_q, t, "y") for t in range(4)]
+        e_rows.append(product(w2_q, 3, "e"))
+        for t in range(3):
+            for h in range(2):
+                gather_e(e_rows[t], t, h * HALF, HALF)
+        for t in range(3):
+            for h in range(2):
+                gather_y(y_rows[t], t, h * HALF, HALF)
+        z = []
+        gather_e(e_rows[3], 3, *EDGE_CHUNKS[0])
+        for c in range(len(EDGE_CHUNKS)):
+            if c + 1 < len(EDGE_CHUNKS):
+                gather_e(e_rows[3], 3, *EDGE_CHUNKS[c + 1])
+            gather_y(y_rows[3], 3, *EDGE_CHUNKS[c])
+            z.append(relu(c))
+        for c in range(len(EDGE_CHUNKS)):
+            finish(c, z[c])

@@ -18,7 +18,7 @@ ADD = mybir.AluOpType.add
 
 P = 128
 HALF = 512
-X_CHUNKS = ((0, 0, 1024, 640), (0, 1024, 1024, 640), (1, 0, 512, 0), (1, 512, 512, 0), (1, 1024, 512, 0), (1, 1536, 512, 320))
+X_CHUNKS = ((0, 0, 1024, 640), (0, 1024, 1024, 640), (1, 0, 512, 0), (1, 512, 512, 0), (1, 1024, 512, 0), (1, 1536, 256, 128), (1, 1792, 256, 128))
 EDGE_CHUNKS = ((0, 256), (256, 256), (512, 256), (768, 128), (896, 128))
 
 
@@ -111,11 +111,14 @@ def tile_picked_hub_relu_e_kernel(tc, xT, w1, w2, w3_words, w3_scales, offs, src
         x_q.append(quantize(x_picked[1][:], HALF, "x1", tag="w2_grouped"))
         w1_grouped = weave_w(w1_raw, "w1")
 
-        def product(w_q, t, name, first=False):
+        def bank_tile(index, width):
+            return psum.tile([P, width], F32, name=f"bank{index}", tag=f"bank{index}")
+
+        def product(w_q, t, name, order, first=False):
             rows = keep.tile([P, S], F32, name=f"{name}{t}")
             cols = slice(t * P, (t + 1) * P)
             for h in range(2):
-                bank = psum.tile([P, HALF], F32, name="bank", tag="bank", bufs=6)
+                bank = bank_tile((2 * order + h) % 6, HALF)
                 nc.tensor.matmul_mx(
                     out=bank[:],
                     lhsT=w_q[0][:, cols].bitcast(FP8X4),
@@ -131,33 +134,32 @@ def tile_picked_hub_relu_e_kernel(tc, xT, w1, w2, w3_words, w3_scales, offs, src
                     nc.scalar.copy(out=rows[:, h * HALF : (h + 1) * HALF], in_=bank[:])
             return rows
 
-        e_picked = [keep.tile([P, S], F32, name=f"e_picked{t}") for t in range(4)]
-        sums = keep.tile([P, 4, S], F32, name="sums")
+        e_picked = [keep.tile([P, S], F32, name=f"e_picked{t}") for t in range(3)]
+        sums = [keep.tile([P, 2, S], F32, name=f"sums{u}") for u in range(2)]
+        z = [keep.tile([P, 4 * width], BF16, name=f"z{c}", align_bytes=64) for c, (r0, width) in enumerate(EDGE_CHUNKS)]
 
-        def gather_e(rows, t, r0, width):
+        def gather_e(picked, rows, r0, width):
             cols = slice(r0 // 16, (r0 + width) // 16)
-            nc.vector.tensor_copy(out=e_picked[t][:, r0 : r0 + width], in_=rows[:].indirect(dst_sb[:, cols]))
+            nc.vector.tensor_copy(out=picked, in_=rows[:].indirect(dst_sb[:, cols]))
 
-        def gather_y(rows, t, r0, width):
+        def gather_y(picked, rows, t, r0, width):
             cols = slice(r0 // 16, (r0 + width) // 16)
             nc.vector.tensor_tensor(
-                out=sums[:, t, r0 : r0 + width], in0=rows[:].indirect(src_sb[:, cols]), in1=e_picked[t][:, r0 : r0 + width], op=ADD
+                out=sums[t // 2][:, t % 2, r0 : r0 + width], in0=rows[:].indirect(src_sb[:, cols]), in1=picked, op=ADD
             )
 
-        def relu(c):
+        def relu(c, u):
             r0, width = EDGE_CHUNKS[c]
-            z = keep.tile([P, 4 * width], BF16, name=f"z{c}", align_bytes=64)
             nc.scalar.activation(
-                out=z[:].rearrange("p (n i t) -> p n t i", i=4, t=4),
-                in_=sums[:, :, r0 : r0 + width].rearrange("p t (n i) -> p n t i", i=4),
+                out=z[c][:].rearrange("p (n t) -> p n t", t=4)[:, :, 2 * u : 2 * u + 2],
+                in_=sums[u][:, :, r0 : r0 + width].rearrange("p t n -> p n t"),
                 func=ACT.Relu,
             )
-            return z
 
-        def finish(c, z):
+        def finish(c):
             r0, width = EDGE_CHUNKS[c]
-            codes, scales = quantize(z[:], width, f"z{c}")
-            bank = psum.tile([P, width], F32, name="out_bank", tag="out_bank", bufs=2)
+            codes, scales = quantize(z[c][:], width, f"z{c}")
+            bank = bank_tile((6 + c) % 8, width)
             nc.tensor.matmul_mx(
                 out=bank[:],
                 lhsT=w3_codes[:].bitcast(FP4X4),
@@ -168,29 +170,34 @@ def tile_picked_hub_relu_e_kernel(tc, xT, w1, w2, w3_words, w3_scales, offs, src
                 stop=True,
             )
             result = keep.tile([P, width], F32, name=f"result{c}")
-            if c == len(EDGE_CHUNKS) - 1:
+            if c in (2, 4):
                 nc.vector.tensor_copy(out=result[:], in_=bank[:])
             else:
                 nc.scalar.copy(out=result[:], in_=bank[:])
             nc.sync.dma_start(out=out[:, r0 : r0 + width], in_=result[:])
 
-        e_rows = [product(w2_q, 0, "e", first=True)]
+        e_rows = [product(w2_q, 0, "e", 0, first=True)]
         w1_q = quantize(w1_grouped[:], H, "w1")
-        e_rows += [product(w2_q, 1, "e"), product(w2_q, 2, "e")]
-        y_rows = [product(w1_q, t, "y") for t in range(4)]
-        e_rows.append(product(w2_q, 3, "e"))
+        e_rows += [product(w2_q, 1, "e", 1), product(w2_q, 2, "e", 2)]
+        y_rows = [product(w1_q, t, "y", 3 + t) for t in range(4)]
+        e_rows.append(product(w2_q, 3, "e", 7))
         for t in range(3):
             for h in range(2):
-                gather_e(e_rows[t], t, h * HALF, HALF)
+                gather_e(e_picked[t][:, h * HALF : (h + 1) * HALF], e_rows[t], h * HALF, HALF)
         for t in range(3):
             for h in range(2):
-                gather_y(y_rows[t], t, h * HALF, HALF)
-        z = []
-        gather_e(e_rows[3], 3, *EDGE_CHUNKS[0])
+                gather_y(e_picked[t][:, h * HALF : (h + 1) * HALF], y_rows[t], t, h * HALF, HALF)
+            if t == 1:
+                for c in range(len(EDGE_CHUNKS)):
+                    relu(c, 0)
+        last = []
+        for c in range(len(EDGE_CHUNKS) + 1):
+            if c < len(EDGE_CHUNKS):
+                r0, width = EDGE_CHUNKS[c]
+                last.append(keep.tile([P, width], F32, name=f"e_last{c}", tag=f"e_last{c % 3}"))
+                gather_e(last[c][:], e_rows[3], r0, width)
+            if c > 0:
+                gather_y(last[c - 1][:], y_rows[3], 3, *EDGE_CHUNKS[c - 1])
+                relu(c - 1, 1)
         for c in range(len(EDGE_CHUNKS)):
-            if c + 1 < len(EDGE_CHUNKS):
-                gather_e(e_rows[3], 3, *EDGE_CHUNKS[c + 1])
-            gather_y(y_rows[3], 3, *EDGE_CHUNKS[c])
-            z.append(relu(c))
-        for c in range(len(EDGE_CHUNKS)):
-            finish(c, z[c])
+            finish(c)

@@ -18,8 +18,18 @@ ADD = mybir.AluOpType.add
 
 P = 128
 HALF = 512
-X_CHUNKS = ((0, 0, 1024, 640), (0, 1024, 1024, 640), (1, 0, 512, 0), (1, 512, 512, 0), (1, 1024, 512, 0), (1, 1536, 256, 128), (1, 1792, 256, 128))
-EDGE_CHUNKS = ((0, 256), (256, 256), (512, 256), (768, 128), (896, 128))
+X_LOADS = (
+    (0, 0, 1024, 640),
+    (0, 1024, 512, 320),
+    (0, 1536, 512, 320),
+    (1, 0, 512, 0),
+    (1, 512, 512, 0),
+    (1, 1024, 512, 0),
+    (1, 1536, 256, 128),
+    (1, 1792, 256, 176),
+)
+NODE_PIECES = ((0, 512), (512, 256), (768, 256))
+EDGE_PIECES = ((0, 256), (256, 256), (512, 256), (768, 128), (896, 128))
 
 
 def tile_picked_hub_relu_e_kernel(tc, xT, w1, w2, w3_words, w3_scales, offs, src, dst, out):
@@ -38,7 +48,7 @@ def tile_picked_hub_relu_e_kernel(tc, xT, w1, w2, w3_words, w3_scales, offs, src
 
         x_rows = xT.rearrange("(p u e) t -> p u e t", u=2, e=2)
         x_raw = []
-        for i, (u, c0, width, vec) in enumerate(X_CHUNKS):
+        for i, (u, c0, width, vec) in enumerate(X_LOADS):
             raw = keep.tile([P, 2, width], F32, name=f"x_raw{i}")
             nc.sync.dma_start(out=raw[:], in_=x_rows[:, u, :, c0 : c0 + width])
             x_raw.append(raw)
@@ -46,17 +56,13 @@ def tile_picked_hub_relu_e_kernel(tc, xT, w1, w2, w3_words, w3_scales, offs, src
                 nc.sync.dma_start(offs_sb[:], offs)
 
         def load_w(w, name):
-            rows = w.rearrange("(p j) c -> p j c", j=4)
-            parts = []
-            for half in range(2):
-                raw = keep.tile([P, 4, H // 2], F32, name=f"{name}_raw{half}", tag=f"{name}_raw{half}")
-                nc.sync.dma_start(out=raw[:], in_=rows[:, :, half * (H // 2) : (half + 1) * (H // 2)])
-                parts.append(raw)
-            return parts
+            raw = keep.tile([P, 4, H], F32, name=f"{name}_raw")
+            nc.sync.dma_start(out=raw[:], in_=w.rearrange("(p j) c -> p j c", j=4))
+            return raw
 
         w2_raw = load_w(w2, "w2")
-        w1_raw = load_w(w1, "w1")
         nc.sync.dma_start(dst_sb[:], dst)
+        w1_raw = load_w(w1, "w1")
         nc.sync.dma_start(src_sb[:], src)
         nc.sync.dma_start(out=w3_codes[:].bitcast(I32), in_=w3_words[0].bitcast(I32))
         for q in range(4):
@@ -66,102 +72,145 @@ def tile_picked_hub_relu_e_kernel(tc, xT, w1, w2, w3_words, w3_scales, offs, src
             )
 
         x_pairs = [keep.tile([P, 2 * T], BF16, name=f"x_pairs{u}") for u in range(2)]
-        x_picked = [keep.tile([P, 4 * HALF], BF16, name=f"x_picked{h}", align_bytes=64) for h in range(2)]
+        x_picked = [keep.tile([P, 4 * width], BF16, name=f"x_picked{i}", align_bytes=64) for i, (n0, width) in enumerate(NODE_PIECES)]
+        x_codes = []
+        x_scales = keep.tile([P, S], U8, name="x_scales", align_bytes=64)
 
         def cast_x(i):
-            u, c0, width, vec = X_CHUNKS[i]
+            u, c0, width, vec = X_LOADS[i]
             pairs = x_pairs[u][:].rearrange("p (t e) -> p t e", e=2)
             raw = x_raw[i][:].rearrange("p e t -> p t e")
             nc.scalar.activation(out=pairs[:, c0 + vec : c0 + width, :], in_=raw[:, vec:width, :], func=ACT.Copy)
             if vec:
                 nc.vector.tensor_copy(out=pairs[:, c0 : c0 + vec, :], in_=raw[:, 0:vec, :])
 
-        def gather_x(u, h):
-            words = x_picked[h][:].bitcast(U32).rearrange("p (n u) -> p n u", u=2)
-            cols = slice(h * HALF // 16, (h + 1) * HALF // 16)
-            nc.vector.tensor_copy(out=words[:, :, u], in_=x_pairs[u][:].bitcast(U32).indirect(offs_sb[:, cols]))
+        def entries(lst, first, count):
+            return lst[:, first // 16 : (first + count) // 16]
 
-        def quantize(values, width, name, tag=None):
-            codes = keep.tile([P, width], U32, name=f"{name}_codes", tag=tag or f"{name}_codes", align_bytes=64)
+        def gather_x(u, i):
+            words = x_picked[i][:].bitcast(U32).rearrange("p (n u) -> p n u", u=2)
+            nc.vector.tensor_copy(out=words[:, :, u], in_=x_pairs[u][:].bitcast(U32).indirect(entries(offs_sb, *NODE_PIECES[i])))
+
+        def x_words(n0, width):
+            return x_codes[n0 // HALF][:, n0 % HALF : n0 % HALF + width].bitcast(FP8X4)
+
+        def quantize_x(i):
+            n0, width = NODE_PIECES[i]
+            nc.vector.quantize_mx(out=x_words(n0, width), scales=x_scales[:, n0 : n0 + width], in_=x_picked[i][:])
+
+        def quantize(values, width, name):
+            codes = keep.tile([P, width], U32, name=f"{name}_codes", align_bytes=64)
             scales = keep.tile([P, width], U8, name=f"{name}_scales", align_bytes=64)
             nc.vector.quantize_mx(out=codes[:].bitcast(FP8X4), scales=scales[:], in_=values)
             return codes, scales
 
-        def weave_w(parts, name):
-            grouped = keep.tile([P, 4 * H], BF16, name=f"{name}_grouped", tag=f"{name}_grouped", align_bytes=64)
-            view = grouped[:].rearrange("p (t m j) -> p m j t", t=4, j=4)
-            for half in range(2):
-                nc.scalar.copy(
-                    out=view[:, half * 64 : (half + 1) * 64],
-                    in_=parts[half][:].rearrange("p j (m t) -> p m j t", t=4),
-                )
+        def weave_w(raw, v, name):
+            grouped = keep.tile([P, 2 * H], BF16, name=f"{name}_grouped{v}", tag=f"{name}_grouped{v}", align_bytes=64)
+            nc.scalar.copy(
+                out=grouped[:].rearrange("p (t m j) -> p m j t", t=2, j=4),
+                in_=raw[:].rearrange("p j (m t) -> p m j t", t=4)[:, :, :, 2 * v : 2 * v + 2],
+            )
             return grouped
 
-        cast_x(0)
-        cast_x(1)
-        gather_x(0, 0)
-        gather_x(0, 1)
-        for i in range(2, len(X_CHUNKS)):
-            cast_x(i)
-        w2_grouped = weave_w(w2_raw, "w2")
-        gather_x(1, 0)
-        gather_x(1, 1)
-        x_q = [quantize(x_picked[0][:], HALF, "x0")]
-        w2_q = quantize(w2_grouped[:], H, "w2")
-        x_q.append(quantize(x_picked[1][:], HALF, "x1", tag="w2_grouped"))
-        w1_grouped = weave_w(w1_raw, "w1")
+        banks = [psum.tile([P, HALF], F32, name=f"bank{b}") for b in range(8)]
 
-        def bank_tile(index, width):
-            return psum.tile([P, width], F32, name=f"bank{index}", tag=f"bank{index}")
-
-        def product(w_q, t, name, order, first=False):
+        def product(w_q, t, name, pieces, where, by_vector=()):
             rows = keep.tile([P, S], F32, name=f"{name}{t}")
-            cols = slice(t * P, (t + 1) * P)
-            for h in range(2):
-                bank = bank_tile((2 * order + h) % 6, HALF)
+            codes, scales = w_q[t // 2]
+            cols = slice(t % 2 * P, (t % 2 + 1) * P)
+            for i, (n0, width) in enumerate(pieces):
+                bank = banks[where[i]][:, 0:width]
                 nc.tensor.matmul_mx(
-                    out=bank[:],
-                    lhsT=w_q[0][:, cols].bitcast(FP8X4),
-                    lhsT_scale=w_q[1][:, cols],
-                    rhs=x_q[h][0][:].bitcast(FP8X4),
-                    rhs_scale=x_q[h][1][:],
+                    out=bank,
+                    lhsT=codes[:, cols].bitcast(FP8X4),
+                    lhsT_scale=scales[:, cols],
+                    rhs=x_words(n0, width),
+                    rhs_scale=x_scales[:, n0 : n0 + width],
                     start=True,
                     stop=True,
                 )
-                if first and h == 0:
-                    nc.vector.tensor_copy(out=rows[:, h * HALF : (h + 1) * HALF], in_=bank[:])
+                if i in by_vector:
+                    nc.vector.tensor_copy(out=rows[:, n0 : n0 + width], in_=bank)
                 else:
-                    nc.scalar.copy(out=rows[:, h * HALF : (h + 1) * HALF], in_=bank[:])
+                    nc.scalar.copy(out=rows[:, n0 : n0 + width], in_=bank)
             return rows
 
-        e_picked = [keep.tile([P, S], F32, name=f"e_picked{t}") for t in range(3)]
-        sums = [keep.tile([P, 2, S], F32, name=f"sums{u}") for u in range(2)]
-        z = [keep.tile([P, 4 * width], BF16, name=f"z{c}", align_bytes=64) for c, (r0, width) in enumerate(EDGE_CHUNKS)]
+        halves = ((0, HALF), (HALF, HALF))
 
-        def gather_e(picked, rows, r0, width):
-            cols = slice(r0 // 16, (r0 + width) // 16)
-            nc.vector.tensor_copy(out=picked, in_=rows[:].indirect(dst_sb[:, cols]))
+        for i in range(3):
+            cast_x(i)
+        for i in range(len(NODE_PIECES)):
+            gather_x(0, i)
+        for i in range(3, len(X_LOADS)):
+            cast_x(i)
+        w2_grouped = [weave_w(w2_raw, v, "w2") for v in range(2)]
+        gather_x(1, 0)
+        gather_x(1, 1)
+        x_codes.append(keep.tile([P, HALF], U32, name="x_codes0", align_bytes=64))
+        quantize_x(0)
+        gather_x(1, 2)
+        w2_q = [quantize(w2_grouped[0][:], H // 2, "w2a")]
+        x_codes.append(keep.tile([P, HALF], U32, name="x_codes1", tag="w2_grouped0", align_bytes=64))
+        quantize_x(1)
+        quantize_x(2)
+        w2_q.append(quantize(w2_grouped[1][:], H // 2, "w2b"))
 
-        def gather_y(picked, rows, t, r0, width):
-            cols = slice(r0 // 16, (r0 + width) // 16)
+        e_picked = {}
+
+        def gather_e(rows, t, r0, width, tag=None):
+            picked = keep.tile([P, width], F32, name=f"e_picked{t}_{r0}", tag=tag or f"e_picked{t}_{r0}")
+            nc.vector.tensor_copy(out=picked[:], in_=rows[:].indirect(entries(dst_sb, r0, width)))
+            for r in range(r0, r0 + width, P):
+                e_picked[t, r] = (picked, r - r0)
+
+        e_rows = [product(w2_q, 0, "e", NODE_PIECES, (0, 1, 2), by_vector=(1, 2))]
+        e_rows.append(product(w2_q, 1, "e", halves, (0, 3)))
+        w1_grouped = [weave_w(w1_raw, 0, "w1")]
+        e_rows.append(product(w2_q, 2, "e", halves, (4, 5)))
+        w1_grouped.append(weave_w(w1_raw, 1, "w1"))
+        e_rows.append(product(w2_q, 3, "e", halves, (6, 7)))
+        for t in range(2):
+            for r0, width in halves:
+                gather_e(e_rows[t], t, r0, width)
+        w1_q = [quantize(w1_grouped[0][:], H // 2, "w1a")]
+        for r0, width in halves:
+            gather_e(e_rows[2], 2, r0, width)
+        w1_q.append(quantize(w1_grouped[1][:], H // 2, "w1b"))
+        gather_e(e_rows[3], 3, 0, 256, tag="sums1")
+        gather_e(e_rows[3], 3, 256, 256, tag="sums2")
+        gather_e(e_rows[3], 3, HALF, HALF)
+        y_rows = [product(w1_q, t, "y", halves, (2 * t, 2 * t + 1)) for t in range(4)]
+
+        z = [keep.tile([P, 4 * width], BF16, name=f"z{c}", align_bytes=64) for c, (r0, width) in enumerate(EDGE_PIECES)]
+
+        def gather_y(sums, t, r0, width):
+            picked, at = e_picked[t, r0]
             nc.vector.tensor_tensor(
-                out=sums[t // 2][:, t % 2, r0 : r0 + width], in0=rows[:].indirect(src_sb[:, cols]), in1=picked, op=ADD
+                out=sums, in0=y_rows[t][:].indirect(entries(src_sb, r0, width)), in1=picked[:, at : at + width], op=ADD
             )
 
-        def relu(c, u):
-            r0, width = EDGE_CHUNKS[c]
-            nc.scalar.activation(
-                out=z[c][:].rearrange("p (n t) -> p n t", t=4)[:, :, 2 * u : 2 * u + 2],
-                in_=sums[u][:, :, r0 : r0 + width].rearrange("p t n -> p n t"),
-                func=ACT.Relu,
-            )
+        all_sums = []
+
+        def edges(c):
+            r0, width = EDGE_PIECES[c]
+            sums = keep.tile([P, 4, width], F32, name=f"sums{c}", tag=f"sums{c % 3}")
+            all_sums.append(sums)
+            rounded = z[c][:].rearrange("p (n t) -> p n t", t=4)
+            step = 2 if c == len(EDGE_PIECES) - 1 else 4
+            for t in range(4):
+                gather_y(sums[:, t, :], t, r0, width)
+                if (t + 1) % step == 0:
+                    planes = slice(t + 1 - step, t + 1)
+                    nc.scalar.activation(
+                        out=rounded[:, :, planes], in_=sums[:, planes, :].rearrange("p t n -> p n t"), func=ACT.Relu
+                    )
 
         def finish(c):
-            r0, width = EDGE_CHUNKS[c]
+            r0, width = EDGE_PIECES[c]
             codes, scales = quantize(z[c][:], width, f"z{c}")
-            bank = bank_tile((6 + c) % 8, width)
+            bank = banks[c][:, 0:width]
             nc.tensor.matmul_mx(
-                out=bank[:],
+                out=bank,
                 lhsT=w3_codes[:].bitcast(FP4X4),
                 lhsT_scale=w3_bytes[:],
                 rhs=codes[:].bitcast(FP8X4),
@@ -170,34 +219,15 @@ def tile_picked_hub_relu_e_kernel(tc, xT, w1, w2, w3_words, w3_scales, offs, src
                 stop=True,
             )
             result = keep.tile([P, width], F32, name=f"result{c}")
-            if c in (2, 4):
-                nc.vector.tensor_copy(out=result[:], in_=bank[:])
+            if c == len(EDGE_PIECES) - 1:
+                nc.vector.tensor_copy(out=result[:], in_=bank)
             else:
-                nc.scalar.copy(out=result[:], in_=bank[:])
+                nc.scalar.copy(out=result[:], in_=bank)
             nc.sync.dma_start(out=out[:, r0 : r0 + width], in_=result[:])
 
-        e_rows = [product(w2_q, 0, "e", 0, first=True)]
-        w1_q = quantize(w1_grouped[:], H, "w1")
-        e_rows += [product(w2_q, 1, "e", 1), product(w2_q, 2, "e", 2)]
-        y_rows = [product(w1_q, t, "y", 3 + t) for t in range(4)]
-        e_rows.append(product(w2_q, 3, "e", 7))
-        for t in range(3):
-            for h in range(2):
-                gather_e(e_picked[t][:, h * HALF : (h + 1) * HALF], e_rows[t], h * HALF, HALF)
-        for t in range(3):
-            for h in range(2):
-                gather_y(e_picked[t][:, h * HALF : (h + 1) * HALF], y_rows[t], t, h * HALF, HALF)
-            if t == 1:
-                for c in range(len(EDGE_CHUNKS)):
-                    relu(c, 0)
-        last = []
-        for c in range(len(EDGE_CHUNKS) + 1):
-            if c < len(EDGE_CHUNKS):
-                r0, width = EDGE_CHUNKS[c]
-                last.append(keep.tile([P, width], F32, name=f"e_last{c}", tag=f"e_last{c % 3}"))
-                gather_e(last[c][:], e_rows[3], r0, width)
-            if c > 0:
-                gather_y(last[c - 1][:], y_rows[3], 3, *EDGE_CHUNKS[c - 1])
-                relu(c - 1, 1)
-        for c in range(len(EDGE_CHUNKS)):
-            finish(c)
+        for c in range(len(EDGE_PIECES)):
+            edges(c)
+            if c > 1:
+                finish(c - 2)
+        finish(len(EDGE_PIECES) - 2)
+        finish(len(EDGE_PIECES) - 1)

@@ -19,15 +19,23 @@ ADD = mybir.AluOpType.add
 P = 128
 HALF = 512
 X_LOADS = (
-    (0, 0, 1024, 640),
-    (0, 1024, 512, 320),
-    (0, 1536, 512, 320),
-    (1, 0, 512, 0),
-    (1, 512, 512, 0),
-    (1, 1024, 512, 0),
-    (1, 1536, 256, 128),
-    (1, 1792, 256, 176),
+    (0, 0, 1024, (1024, 0, 0)),
+    (0, 1024, 1024, (704, 320, 0)),
+    (1, 0, 512, (0, 0, 512)),
+    (1, 512, 512, (0, 0, 512)),
+    (1, 1024, 512, (0, 0, 512)),
+    (1, 1536, 512, (0, 512, 0)),
+    (2, 0, 512, (0, 0, 512)),
+    (2, 512, 512, (0, 0, 512)),
+    (2, 1024, 512, (0, 0, 512)),
+    (2, 1536, 512, (0, 512, 0)),
+    (3, 0, 512, (0, 0, 512)),
+    (3, 512, 512, (0, 0, 512)),
+    (3, 1024, 512, (0, 0, 512)),
+    (3, 1536, 256, (0, 256, 0)),
+    (3, 1792, 256, (0, 256, 0)),
 )
+VECTOR_ENTRIES = (640, 640, 576, 576)
 NODE_PIECES = ((0, 512), (512, 256), (768, 256))
 EDGE_PIECES = ((0, 256), (256, 256), (512, 256), (768, 128), (896, 128))
 
@@ -46,13 +54,11 @@ def tile_picked_hub_relu_e_kernel(tc, xT, w1, w2, w3_words, w3_scales, offs, src
         w3_codes = keep.tile([P, 2 * N], U8, name="w3_codes", align_bytes=64)
         nc.vector.memset(w3_bytes[:].bitcast(I32), 0)
 
-        x_rows = xT.rearrange("(p u e) t -> p u e t", u=2, e=2)
-        x_raw = []
-        for i, (u, c0, width, vec) in enumerate(X_LOADS):
-            raw = keep.tile([P, 2, width], F32, name=f"x_raw{i}")
-            nc.sync.dma_start(out=raw[:], in_=x_rows[:, u, :, c0 : c0 + width])
-            x_raw.append(raw)
-            if i == 1:
+        x_rows = xT.rearrange("(p j) t -> p j t", j=4)
+        x_raw = [keep.tile([P, T], F32, name=f"x_raw{j}") for j in range(4)]
+        for i, (j, c0, width, vec) in enumerate(X_LOADS):
+            nc.sync.dma_start(out=x_raw[j][:, c0 : c0 + width], in_=x_rows[:, j, c0 : c0 + width])
+            if i == 0:
                 nc.sync.dma_start(offs_sb[:], offs)
 
         def load_w(w, name):
@@ -71,32 +77,36 @@ def tile_picked_hub_relu_e_kernel(tc, xT, w1, w2, w3_words, w3_scales, offs, src
                 in_=w3_scales[0, 4 * q : 4 * q + 4, :].bitcast(I32),
             )
 
-        x_pairs = [keep.tile([P, 2 * T], BF16, name=f"x_pairs{u}") for u in range(2)]
-        x_picked = [keep.tile([P, 4 * width], BF16, name=f"x_picked{i}", align_bytes=64) for i, (n0, width) in enumerate(NODE_PIECES)]
+        x_half = [keep.tile([P, T], BF16, name=f"x_half{j}") for j in range(4)]
+        x_picked = keep.tile([P, 4 * S], BF16, name="x_picked", align_bytes=64)
         x_codes = []
         x_scales = keep.tile([P, S], U8, name="x_scales", align_bytes=64)
 
         def cast_x(i):
-            u, c0, width, vec = X_LOADS[i]
-            pairs = x_pairs[u][:].rearrange("p (t e) -> p t e", e=2)
-            raw = x_raw[i][:].rearrange("p e t -> p t e")
-            nc.scalar.activation(out=pairs[:, c0 + vec : c0 + width, :], in_=raw[:, vec:width, :], func=ACT.Copy)
-            if vec:
-                nc.vector.tensor_copy(out=pairs[:, c0 : c0 + vec, :], in_=raw[:, 0:vec, :])
+            j, c0, width, shares = X_LOADS[i]
+            for count, copy in zip(shares, (nc.vector.tensor_copy, nc.scalar.copy, nc.gpsimd.tensor_copy)):
+                if count:
+                    copy(out=x_half[j][:, c0 : c0 + count], in_=x_raw[j][:, c0 : c0 + count])
+                c0 += count
 
         def entries(lst, first, count):
             return lst[:, first // 16 : (first + count) // 16]
 
-        def gather_x(u, i):
-            words = x_picked[i][:].bitcast(U32).rearrange("p (n u) -> p n u", u=2)
-            nc.vector.tensor_copy(out=words[:, :, u], in_=x_pairs[u][:].bitcast(U32).indirect(entries(offs_sb, *NODE_PIECES[i])))
+        def gather_x(j, pieces):
+            planes = x_picked[:].rearrange("p (n j) -> p n j", j=4)
+            mine = VECTOR_ENTRIES[j]
+            nc.vector.tensor_copy(out=planes[:, 0:mine, j], in_=x_raw[j][:].indirect(entries(offs_sb, 0, mine)))
+            for n0, width in pieces:
+                nc.scalar.activation(
+                    out=planes[:, n0 : n0 + width, j], in_=x_half[j][:].indirect(entries(offs_sb, n0, width)), func=ACT.Copy
+                )
 
         def x_words(n0, width):
             return x_codes[n0 // HALF][:, n0 % HALF : n0 % HALF + width].bitcast(FP8X4)
 
         def quantize_x(i):
             n0, width = NODE_PIECES[i]
-            nc.vector.quantize_mx(out=x_words(n0, width), scales=x_scales[:, n0 : n0 + width], in_=x_picked[i][:])
+            nc.vector.quantize_mx(out=x_words(n0, width), scales=x_scales[:, n0 : n0 + width], in_=x_picked[:, 4 * n0 : 4 * (n0 + width)])
 
         def quantize(values, width, name):
             codes = keep.tile([P, width], U32, name=f"{name}_codes", align_bytes=64)
@@ -104,26 +114,30 @@ def tile_picked_hub_relu_e_kernel(tc, xT, w1, w2, w3_words, w3_scales, offs, src
             nc.vector.quantize_mx(out=codes[:].bitcast(FP8X4), scales=scales[:], in_=values)
             return codes, scales
 
-        def weave_w(raw, v, name):
-            grouped = keep.tile([P, 2 * H], BF16, name=f"{name}_grouped{v}", tag=f"{name}_grouped{v}", align_bytes=64)
-            nc.scalar.copy(
-                out=grouped[:].rearrange("p (t m j) -> p m j t", t=2, j=4),
-                in_=raw[:].rearrange("p j (m t) -> p m j t", t=4)[:, :, :, 2 * v : 2 * v + 2],
-            )
+        def weave_w(raw, first, count, name, on_vector=0):
+            grouped = keep.tile([P, count * H], BF16, name=f"{name}_grouped{first}", tag=f"{name}_grouped{first}", align_bytes=64)
+            dealt = grouped[:].rearrange("p (t m j) -> p m j t", t=count, j=4)
+            columns = raw[:].rearrange("p j (m t) -> p m j t", t=4)[:, :, :, first : first + count]
+            nc.scalar.copy(out=dealt[:, on_vector:P], in_=columns[:, on_vector:P])
+            if on_vector:
+                nc.vector.tensor_copy(out=dealt[:, 0:on_vector], in_=columns[:, 0:on_vector])
             return grouped
+
+        def quantize_w(grouped, count, name):
+            codes, scales = quantize(grouped[:], count * P, name)
+            return [(codes[:, t * P : (t + 1) * P], scales[:, t * P : (t + 1) * P]) for t in range(count)]
 
         banks = [psum.tile([P, HALF], F32, name=f"bank{b}") for b in range(8)]
 
         def product(w_q, t, name, pieces, where, by_vector=()):
             rows = keep.tile([P, S], F32, name=f"{name}{t}")
-            codes, scales = w_q[t // 2]
-            cols = slice(t % 2 * P, (t % 2 + 1) * P)
+            codes, scales = w_q[t]
             for i, (n0, width) in enumerate(pieces):
                 bank = banks[where[i]][:, 0:width]
                 nc.tensor.matmul_mx(
                     out=bank,
-                    lhsT=codes[:, cols].bitcast(FP8X4),
-                    lhsT_scale=scales[:, cols],
+                    lhsT=codes.bitcast(FP8X4),
+                    lhsT_scale=scales,
                     rhs=x_words(n0, width),
                     rhs_scale=x_scales[:, n0 : n0 + width],
                     start=True,
@@ -137,23 +151,19 @@ def tile_picked_hub_relu_e_kernel(tc, xT, w1, w2, w3_words, w3_scales, offs, src
 
         halves = ((0, HALF), (HALF, HALF))
 
-        for i in range(3):
-            cast_x(i)
-        for i in range(len(NODE_PIECES)):
-            gather_x(0, i)
-        for i in range(3, len(X_LOADS)):
-            cast_x(i)
-        w2_grouped = [weave_w(w2_raw, v, "w2") for v in range(2)]
-        gather_x(1, 0)
-        gather_x(1, 1)
+        for j in range(4):
+            for i in range(len(X_LOADS)):
+                if X_LOADS[i][0] == j:
+                    cast_x(i)
+            gather_x(j, ((VECTOR_ENTRIES[j], S - VECTOR_ENTRIES[j]),))
         x_codes.append(keep.tile([P, HALF], U32, name="x_codes0", align_bytes=64))
         quantize_x(0)
-        gather_x(1, 2)
-        w2_q = [quantize(w2_grouped[0][:], H // 2, "w2a")]
+        w2_first = weave_w(w2_raw, 0, 1, "w2", on_vector=P // 2)
+        w2_second = weave_w(w2_raw, 1, 1, "w2")
+        w2_q = quantize_w(w2_first, 1, "w2a")
         x_codes.append(keep.tile([P, HALF], U32, name="x_codes1", tag="w2_grouped0", align_bytes=64))
         quantize_x(1)
         quantize_x(2)
-        w2_q.append(quantize(w2_grouped[1][:], H // 2, "w2b"))
 
         e_picked = {}
 
@@ -163,19 +173,23 @@ def tile_picked_hub_relu_e_kernel(tc, xT, w1, w2, w3_words, w3_scales, offs, src
             for r in range(r0, r0 + width, P):
                 e_picked[t, r] = (picked, r - r0)
 
-        e_rows = [product(w2_q, 0, "e", NODE_PIECES, (0, 1, 2), by_vector=(1, 2))]
+        e_rows = [product(w2_q, 0, "e", NODE_PIECES, (0, 1, 2), by_vector=(0,))]
+        w2_q += quantize_w(w2_second, 1, "w2b")
         e_rows.append(product(w2_q, 1, "e", halves, (0, 3)))
-        w1_grouped = [weave_w(w1_raw, 0, "w1")]
+        w2_rest = weave_w(w2_raw, 2, 2, "w2")
+        gather_e(e_rows[0], 0, 0, HALF)
+        w2_q += quantize_w(w2_rest, 2, "w2c")
+        gather_e(e_rows[0], 0, HALF, HALF)
+        w1_grouped = [weave_w(w1_raw, 0, 2, "w1")]
         e_rows.append(product(w2_q, 2, "e", halves, (4, 5)))
-        w1_grouped.append(weave_w(w1_raw, 1, "w1"))
+        w1_grouped.append(weave_w(w1_raw, 2, 2, "w1"))
         e_rows.append(product(w2_q, 3, "e", halves, (6, 7)))
-        for t in range(2):
-            for r0, width in halves:
-                gather_e(e_rows[t], t, r0, width)
-        w1_q = [quantize(w1_grouped[0][:], H // 2, "w1a")]
+        for r0, width in halves:
+            gather_e(e_rows[1], 1, r0, width)
+        w1_q = quantize_w(w1_grouped[0], 2, "w1a")
         for r0, width in halves:
             gather_e(e_rows[2], 2, r0, width)
-        w1_q.append(quantize(w1_grouped[1][:], H // 2, "w1b"))
+        w1_q += quantize_w(w1_grouped[1], 2, "w1b")
         gather_e(e_rows[3], 3, 0, 256, tag="sums1")
         gather_e(e_rows[3], 3, 256, 256, tag="sums2")
         gather_e(e_rows[3], 3, HALF, HALF)

@@ -109,22 +109,21 @@ def tile_picked_hub_relu_e_kernel(tc, xT, w1, w2, w3_words, w3_scales, offs, src
             nc.vector.quantize_mx(out=x_words(n0, width), scales=x_scales[:, n0 : n0 + width], in_=x_picked[:, 4 * n0 : 4 * (n0 + width)])
 
         def quantize(values, width, name):
-            codes = keep.tile([P, width], U32, name=f"{name}_codes", align_bytes=64)
+            codes = keep.tile([P, width], U32, name=f"{name}_codes", tag=f"{name}_codes", align_bytes=64)
             scales = keep.tile([P, width], U8, name=f"{name}_scales", align_bytes=64)
             nc.vector.quantize_mx(out=codes[:].bitcast(FP8X4), scales=scales[:], in_=values)
             return codes, scales
 
-        def weave_w(raw, first, count, name, on_vector=0):
-            grouped = keep.tile([P, count * H], BF16, name=f"{name}_grouped{first}", tag=f"{name}_grouped{first}", align_bytes=64)
-            dealt = grouped[:].rearrange("p (t m j) -> p m j t", t=count, j=4)
-            columns = raw[:].rearrange("p j (m t) -> p m j t", t=4)[:, :, :, first : first + count]
-            nc.scalar.copy(out=dealt[:, on_vector:P], in_=columns[:, on_vector:P])
-            if on_vector:
-                nc.vector.tensor_copy(out=dealt[:, 0:on_vector], in_=columns[:, 0:on_vector])
+        def weave_w(copy, raw, first, count, name, tag=None):
+            grouped = keep.tile([P, count * H], BF16, name=f"{name}_grouped{first}", tag=tag or f"{name}_grouped{first}", align_bytes=64)
+            copy(
+                out=grouped[:].rearrange("p (t m j) -> p m j t", t=count, j=4),
+                in_=raw[:].rearrange("p j (m t) -> p m j t", t=4)[:, :, :, first : first + count],
+            )
             return grouped
 
         def quantize_w(grouped, count, name):
-            codes, scales = quantize(grouped[:], count * P, name)
+            codes, scales = quantize(grouped, count * P, name)
             return [(codes[:, t * P : (t + 1) * P], scales[:, t * P : (t + 1) * P]) for t in range(count)]
 
         banks = [psum.tile([P, HALF], F32, name=f"bank{b}") for b in range(8)]
@@ -158,9 +157,9 @@ def tile_picked_hub_relu_e_kernel(tc, xT, w1, w2, w3_words, w3_scales, offs, src
             gather_x(j, ((VECTOR_ENTRIES[j], S - VECTOR_ENTRIES[j]),))
         x_codes.append(keep.tile([P, HALF], U32, name="x_codes0", align_bytes=64))
         quantize_x(0)
-        w2_first = weave_w(w2_raw, 0, 1, "w2", on_vector=P // 2)
-        w2_second = weave_w(w2_raw, 1, 1, "w2")
-        w2_q = quantize_w(w2_first, 1, "w2a")
+        w2_first = weave_w(nc.vector.tensor_copy, w2_raw, 0, 1, "w2")
+        w2_rest = weave_w(nc.scalar.copy, w2_raw, 1, 3, "w2")
+        w2_q = quantize_w(w2_first[:], 1, "w2a")
         x_codes.append(keep.tile([P, HALF], U32, name="x_codes1", tag="w2_grouped0", align_bytes=64))
         quantize_x(1)
         quantize_x(2)
@@ -168,28 +167,24 @@ def tile_picked_hub_relu_e_kernel(tc, xT, w1, w2, w3_words, w3_scales, offs, src
         e_picked = {}
 
         def gather_e(rows, t, r0, width, tag=None):
-            picked = keep.tile([P, width], F32, name=f"e_picked{t}_{r0}", tag=tag or f"e_picked{t}_{r0}")
+            picked = keep.tile([P, width], F32, name=f"e_picked{t}_{r0}", tag=tag or f"e_picked{t}_{r0}", align_bytes=64)
             nc.vector.tensor_copy(out=picked[:], in_=rows[:].indirect(entries(dst_sb, r0, width)))
             for r in range(r0, r0 + width, P):
                 e_picked[t, r] = (picked, r - r0)
 
         e_rows = [product(w2_q, 0, "e", NODE_PIECES, (0, 1, 2), by_vector=(0,))]
-        w2_q += quantize_w(w2_second, 1, "w2b")
+        w2_q += quantize_w(w2_rest[:, 0:H], 1, "w2b")
+        w2_q += quantize_w(w2_rest[:, H : 3 * H], 2, "w2c")
         e_rows.append(product(w2_q, 1, "e", halves, (0, 3)))
-        w2_rest = weave_w(w2_raw, 2, 2, "w2")
-        gather_e(e_rows[0], 0, 0, HALF)
-        w2_q += quantize_w(w2_rest, 2, "w2c")
-        gather_e(e_rows[0], 0, HALF, HALF)
-        w1_grouped = [weave_w(w1_raw, 0, 2, "w1")]
+        w1_grouped = weave_w(nc.scalar.copy, w1_raw, 0, 4, "w1", tag="w2b_codes")
+        for t in range(2):
+            for r0, width in halves:
+                gather_e(e_rows[t], t, r0, width)
         e_rows.append(product(w2_q, 2, "e", halves, (4, 5)))
-        w1_grouped.append(weave_w(w1_raw, 2, 2, "w1"))
         e_rows.append(product(w2_q, 3, "e", halves, (6, 7)))
-        for r0, width in halves:
-            gather_e(e_rows[1], 1, r0, width)
-        w1_q = quantize_w(w1_grouped[0], 2, "w1a")
-        for r0, width in halves:
-            gather_e(e_rows[2], 2, r0, width)
-        w1_q += quantize_w(w1_grouped[1], 2, "w1b")
+        w1_q = quantize_w(w1_grouped[:], 4, "w1")
+        gather_e(e_rows[2], 2, 0, HALF, tag="w2b_codes")
+        gather_e(e_rows[2], 2, HALF, HALF)
         gather_e(e_rows[3], 3, 0, 256, tag="sums1")
         gather_e(e_rows[3], 3, 256, 256, tag="sums2")
         gather_e(e_rows[3], 3, HALF, HALF)
@@ -207,7 +202,7 @@ def tile_picked_hub_relu_e_kernel(tc, xT, w1, w2, w3_words, w3_scales, offs, src
 
         def edges(c):
             r0, width = EDGE_PIECES[c]
-            sums = keep.tile([P, 4, width], F32, name=f"sums{c}", tag=f"sums{c % 3}")
+            sums = keep.tile([P, 4, width], F32, name=f"sums{c}", tag=f"sums{c % 3}", align_bytes=64)
             all_sums.append(sums)
             rounded = z[c][:].rearrange("p (n t) -> p n t", t=4)
             step = 2 if c == len(EDGE_PIECES) - 1 else 4

@@ -44,6 +44,7 @@ def tile_picked_hub_relu_e_kernel(tc, xT, w1, w2, w3_words, w3_scales, offs, src
     nc = tc.nc
     with ExitStack() as ctx:
         keep = ctx.enter_context(tc.tile_pool(name="keep", bufs=1))
+        shared = ctx.enter_context(tc.tile_pool(name="shared", bufs=1))
         psum = ctx.enter_context(tc.psum_pool(name="psum", bufs=1))
 
         offs_sb = keep.tile([P, S // 16], U16, name="offs_sb")
@@ -186,11 +187,15 @@ def tile_picked_hub_relu_e_kernel(tc, xT, w1, w2, w3_words, w3_scales, offs, src
         gather_e(e_rows[2], 2, 0, HALF, tag="w2b_codes")
         gather_e(e_rows[2], 2, HALF, HALF)
         gather_e(e_rows[3], 3, 0, 256, tag="sums1")
-        gather_e(e_rows[3], 3, 256, 256, tag="sums2")
-        gather_e(e_rows[3], 3, HALF, HALF)
+        gather_e(e_rows[3], 3, 256, 768)
         y_rows = [product(w1_q, t, "y", halves, (2 * t, 2 * t + 1)) for t in range(4)]
 
-        z = [keep.tile([P, 4 * width], BF16, name=f"z{c}", align_bytes=64) for c, (r0, width) in enumerate(EDGE_PIECES)]
+        z = [
+            shared.tile([P, 4 * width], BF16, name=f"z{c}", align_bytes=64, offset=0)
+            if c == 1
+            else keep.tile([P, 4 * width], BF16, name=f"z{c}", align_bytes=64)
+            for c, (r0, width) in enumerate(EDGE_PIECES)
+        ]
 
         def gather_y(sums, t, r0, width):
             picked, at = e_picked[t, r0]
@@ -202,16 +207,21 @@ def tile_picked_hub_relu_e_kernel(tc, xT, w1, w2, w3_words, w3_scales, offs, src
 
         def edges(c):
             r0, width = EDGE_PIECES[c]
-            sums = keep.tile([P, 4, width], F32, name=f"sums{c}", tag=f"sums{c % 3}", align_bytes=64)
+            if c == len(EDGE_PIECES) - 1:
+                sums = shared.tile([P, 4, width], F32, name="sums_last", align_bytes=64, offset=0)
+            else:
+                sums = keep.tile([P, 4, width], F32, name=f"sums{c}", tag=f"sums{c % 2}", align_bytes=64)
             all_sums.append(sums)
-            rounded = z[c][:].rearrange("p (n t) -> p n t", t=4)
+            rounded = z[c][:].rearrange("p (c i t) -> p c t i", i=4, t=4)
             step = 2 if c == len(EDGE_PIECES) - 1 else 4
             for t in range(4):
                 gather_y(sums[:, t, :], t, r0, width)
                 if (t + 1) % step == 0:
                     planes = slice(t + 1 - step, t + 1)
                     nc.scalar.activation(
-                        out=rounded[:, :, planes], in_=sums[:, planes, :].rearrange("p t n -> p n t"), func=ACT.Relu
+                        out=rounded[:, :, planes, :],
+                        in_=sums[:, planes, :].rearrange("p t (c i) -> p c t i", i=4),
+                        func=ACT.Relu,
                     )
 
         def finish(c):
@@ -234,9 +244,13 @@ def tile_picked_hub_relu_e_kernel(tc, xT, w1, w2, w3_words, w3_scales, offs, src
                 nc.scalar.copy(out=result[:], in_=bank)
             nc.sync.dma_start(out=out[:, r0 : r0 + width], in_=result[:])
 
-        for c in range(len(EDGE_PIECES)):
-            edges(c)
-            if c > 1:
-                finish(c - 2)
+        edges(0)
+        edges(1)
+        finish(0)
+        edges(2)
+        finish(1)
+        edges(3)
+        edges(4)
+        finish(2)
         finish(len(EDGE_PIECES) - 2)
         finish(len(EDGE_PIECES) - 1)

@@ -19,23 +19,16 @@ ADD = mybir.AluOpType.add
 P = 128
 HALF = 512
 X_LOADS = (
-    (0, 0, 1024, (1024, 0, 0)),
-    (0, 1024, 1024, (704, 320, 0)),
-    (1, 0, 512, (0, 0, 512)),
-    (1, 512, 512, (0, 0, 512)),
-    (1, 1024, 512, (0, 0, 512)),
-    (1, 1536, 512, (0, 512, 0)),
-    (2, 0, 512, (0, 0, 512)),
-    (2, 512, 512, (0, 0, 512)),
-    (2, 1024, 512, (0, 0, 512)),
-    (2, 1536, 512, (0, 512, 0)),
-    (3, 0, 512, (0, 0, 512)),
-    (3, 512, 512, (0, 0, 512)),
+    (0, 0, 2048, (1408, 640, 0)),
+    (1, 0, 1024, (0, 0, 1024)),
+    (1, 1024, 1024, (0, 512, 512)),
+    (2, 0, 1024, (0, 0, 1024)),
+    (2, 1024, 1024, (0, 512, 512)),
+    (3, 0, 1024, (0, 0, 1024)),
     (3, 1024, 512, (0, 0, 512)),
-    (3, 1536, 256, (0, 256, 0)),
-    (3, 1792, 256, (0, 256, 0)),
+    (3, 1536, 512, (0, 512, 0)),
 )
-VECTOR_ENTRIES = (640, 640, 576, 576)
+VECTOR_ENTRIES = (640, 640, 512, 512)
 NODE_PIECES = ((0, 512), (512, 256), (768, 256))
 EDGE_PIECES = ((0, 256), (256, 256), (512, 256), (768, 128), (896, 128))
 
@@ -158,9 +151,9 @@ def tile_picked_hub_relu_e_kernel(tc, xT, w1, w2, w3_words, w3_scales, offs, src
             gather_x(j, ((VECTOR_ENTRIES[j], S - VECTOR_ENTRIES[j]),))
         x_codes.append(keep.tile([P, HALF], U32, name="x_codes0", align_bytes=64))
         quantize_x(0)
-        w2_first = weave_w(nc.vector.tensor_copy, w2_raw, 0, 1, "w2")
-        w2_rest = weave_w(nc.scalar.copy, w2_raw, 1, 3, "w2")
-        w2_q = quantize_w(w2_first[:], 1, "w2a")
+        w2_first = weave_w(nc.vector.tensor_copy, w2_raw, 0, 2, "w2")
+        w2_rest = weave_w(nc.scalar.copy, w2_raw, 2, 2, "w2")
+        w2_q = quantize_w(w2_first[:], 2, "w2a")
         x_codes.append(keep.tile([P, HALF], U32, name="x_codes1", tag="w2_grouped0", align_bytes=64))
         quantize_x(1)
         quantize_x(2)
@@ -174,17 +167,16 @@ def tile_picked_hub_relu_e_kernel(tc, xT, w1, w2, w3_words, w3_scales, offs, src
                 e_picked[t, r] = (picked, r - r0)
 
         e_rows = [product(w2_q, 0, "e", NODE_PIECES, (0, 1, 2), by_vector=(0,))]
-        w2_q += quantize_w(w2_rest[:, 0:H], 1, "w2b")
-        w2_q += quantize_w(w2_rest[:, H : 3 * H], 2, "w2c")
+        w2_q += quantize_w(w2_rest[:], 2, "w2b")
         e_rows.append(product(w2_q, 1, "e", halves, (0, 3)))
-        w1_grouped = weave_w(nc.scalar.copy, w1_raw, 0, 4, "w1", tag="w2b_codes")
+        w1_grouped = weave_w(nc.scalar.copy, w1_raw, 0, 4, "w1", tag="w2a_codes")
         for t in range(2):
             for r0, width in halves:
                 gather_e(e_rows[t], t, r0, width)
         e_rows.append(product(w2_q, 2, "e", halves, (4, 5)))
         e_rows.append(product(w2_q, 3, "e", halves, (6, 7)))
         w1_q = quantize_w(w1_grouped[:], 4, "w1")
-        gather_e(e_rows[2], 2, 0, HALF, tag="w2b_codes")
+        gather_e(e_rows[2], 2, 0, HALF, tag="w2a_codes")
         gather_e(e_rows[2], 2, HALF, HALF)
         gather_e(e_rows[3], 3, 0, 256, tag="sums1")
         gather_e(e_rows[3], 3, 256, 768)

@@ -25,8 +25,7 @@ X_LOADS = (
     (2, 0, 1024, (0, 0, 1024)),
     (2, 1024, 1024, (0, 512, 512)),
     (3, 0, 1024, (0, 0, 1024)),
-    (3, 1024, 512, (0, 0, 512)),
-    (3, 1536, 512, (0, 512, 0)),
+    (3, 1024, 1024, (0, 512, 512)),
 )
 VECTOR_ENTRIES = (640, 640, 512, 512)
 NODE_PIECES = ((0, 512), (512, 256), (768, 256))
@@ -102,22 +101,27 @@ def tile_picked_hub_relu_e_kernel(tc, xT, w1, w2, w3_words, w3_scales, offs, src
             n0, width = NODE_PIECES[i]
             nc.vector.quantize_mx(out=x_words(n0, width), scales=x_scales[:, n0 : n0 + width], in_=x_picked[:, 4 * n0 : 4 * (n0 + width)])
 
-        def quantize(values, width, name):
-            codes = keep.tile([P, width], U32, name=f"{name}_codes", tag=f"{name}_codes", align_bytes=64)
+        def tile_at(shape, dtype, name, offset):
+            if offset is None:
+                return keep.tile(shape, dtype, name=name, tag=name, align_bytes=64)
+            return shared.tile(shape, dtype, name=name, align_bytes=64, offset=offset)
+
+        def quantize(values, width, name, offset=None):
+            codes = tile_at([P, width], U32, f"{name}_codes", offset)
             scales = keep.tile([P, width], U8, name=f"{name}_scales", align_bytes=64)
             nc.vector.quantize_mx(out=codes[:].bitcast(FP8X4), scales=scales[:], in_=values)
             return codes, scales
 
-        def weave_w(copy, raw, first, count, name, tag=None):
-            grouped = keep.tile([P, count * H], BF16, name=f"{name}_grouped{first}", tag=tag or f"{name}_grouped{first}", align_bytes=64)
+        def weave_w(copy, raw, first, count, name, offset=None):
+            grouped = tile_at([P, count * H], BF16, f"{name}_grouped{first}", offset)
             copy(
                 out=grouped[:].rearrange("p (t m j) -> p m j t", t=count, j=4),
                 in_=raw[:].rearrange("p j (m t) -> p m j t", t=4)[:, :, :, first : first + count],
             )
             return grouped
 
-        def quantize_w(grouped, count, name):
-            codes, scales = quantize(grouped, count * P, name)
+        def quantize_w(grouped, count, name, offset=None):
+            codes, scales = quantize(grouped, count * P, name, offset)
             return [(codes[:, t * P : (t + 1) * P], scales[:, t * P : (t + 1) * P]) for t in range(count)]
 
         banks = [psum.tile([P, HALF], F32, name=f"bank{b}") for b in range(8)]
@@ -153,7 +157,7 @@ def tile_picked_hub_relu_e_kernel(tc, xT, w1, w2, w3_words, w3_scales, offs, src
         quantize_x(0)
         w2_first = weave_w(nc.vector.tensor_copy, w2_raw, 0, 2, "w2")
         w2_rest = weave_w(nc.scalar.copy, w2_raw, 2, 2, "w2")
-        w2_q = quantize_w(w2_first[:], 2, "w2a")
+        w2_q = quantize_w(w2_first[:], 2, "w2a", offset=8192 + 1536)
         x_codes.append(keep.tile([P, HALF], U32, name="x_codes1", tag="w2_grouped0", align_bytes=64))
         quantize_x(1)
         quantize_x(2)
@@ -169,22 +173,25 @@ def tile_picked_hub_relu_e_kernel(tc, xT, w1, w2, w3_words, w3_scales, offs, src
         e_rows = [product(w2_q, 0, "e", NODE_PIECES, (0, 1, 2), by_vector=(0,))]
         w2_q += quantize_w(w2_rest[:], 2, "w2b")
         e_rows.append(product(w2_q, 1, "e", halves, (0, 3)))
-        w1_grouped = weave_w(nc.scalar.copy, w1_raw, 0, 4, "w1", tag="w2a_codes")
+        w1_grouped = [weave_w(nc.scalar.copy, w1_raw, 0, 2, "w1", offset=8192)]
+        e_rows.append(product(w2_q, 2, "e", halves, (4, 5)))
+        w1_grouped.append(weave_w(nc.scalar.copy, w1_raw, 2, 2, "w1", offset=8192 + 2048))
+        e_rows.append(product(w2_q, 3, "e", halves, (6, 7)))
         for t in range(2):
             for r0, width in halves:
                 gather_e(e_rows[t], t, r0, width)
-        e_rows.append(product(w2_q, 2, "e", halves, (4, 5)))
-        e_rows.append(product(w2_q, 3, "e", halves, (6, 7)))
-        w1_q = quantize_w(w1_grouped[:], 4, "w1")
-        gather_e(e_rows[2], 2, 0, HALF, tag="w2a_codes")
-        gather_e(e_rows[2], 2, HALF, HALF)
+        w1_q = quantize_w(w1_grouped[0][:], 2, "w1a")
+        for r0, width in halves:
+            gather_e(e_rows[2], 2, r0, width)
+        w1_q += quantize_w(w1_grouped[1][:], 2, "w1b")
         gather_e(e_rows[3], 3, 0, 256, tag="sums1")
         gather_e(e_rows[3], 3, 256, 768)
         y_rows = [product(w1_q, t, "y", halves, (2 * t, 2 * t + 1)) for t in range(4)]
 
+        places = {1: 0, 2: 2048, 4: 2048, 3: 4096}
         z = [
-            shared.tile([P, 4 * width], BF16, name=f"z{c}", align_bytes=64, offset=0)
-            if c == 1
+            shared.tile([P, 4 * width], BF16, name=f"z{c}", align_bytes=64, offset=places[c])
+            if c in places
             else keep.tile([P, 4 * width], BF16, name=f"z{c}", align_bytes=64)
             for c, (r0, width) in enumerate(EDGE_PIECES)
         ]
@@ -204,21 +211,20 @@ def tile_picked_hub_relu_e_kernel(tc, xT, w1, w2, w3_words, w3_scales, offs, src
             else:
                 sums = keep.tile([P, 4, width], F32, name=f"sums{c}", tag=f"sums{c % 2}", align_bytes=64)
             all_sums.append(sums)
-            rounded = z[c][:].rearrange("p (c i t) -> p c t i", i=4, t=4)
-            step = 2 if c == len(EDGE_PIECES) - 1 else 4
             for t in range(4):
                 gather_y(sums[:, t, :], t, r0, width)
-                if (t + 1) % step == 0:
-                    planes = slice(t + 1 - step, t + 1)
-                    nc.scalar.activation(
-                        out=rounded[:, :, planes, :],
-                        in_=sums[:, planes, :].rearrange("p t (c i) -> p c t i", i=4),
-                        func=ACT.Relu,
-                    )
+
+        def relu(c):
+            rounded = z[c][:].rearrange("p (c i t) -> p c t i", i=4, t=4)
+            planes = all_sums[c][:].rearrange("p t (c i) -> p c t i", i=4)
+            if c == len(EDGE_PIECES) - 1:
+                nc.vector.tensor_scalar_max(out=z[c][:].rearrange("p (n t) -> p n t", t=4), in0=all_sums[c][:].rearrange("p t n -> p n t"), scalar1=0.0)
+            else:
+                nc.scalar.activation(out=rounded, in_=planes, func=ACT.Relu)
 
         def finish(c):
             r0, width = EDGE_PIECES[c]
-            codes, scales = quantize(z[c][:], width, f"z{c}")
+            codes, scales = quantize(z[c][:], width, f"z{c}", places[3] if c == len(EDGE_PIECES) - 1 else None)
             bank = banks[c][:, 0:width]
             nc.tensor.matmul_mx(
                 out=bank,
@@ -237,12 +243,17 @@ def tile_picked_hub_relu_e_kernel(tc, xT, w1, w2, w3_words, w3_scales, offs, src
             nc.sync.dma_start(out=out[:, r0 : r0 + width], in_=result[:])
 
         edges(0)
+        relu(0)
         edges(1)
+        relu(1)
         finish(0)
         edges(2)
+        relu(2)
         finish(1)
         edges(3)
+        relu(3)
         edges(4)
         finish(2)
+        relu(4)
         finish(len(EDGE_PIECES) - 2)
         finish(len(EDGE_PIECES) - 1)

@@ -17,19 +17,43 @@ ACT = mybir.ActivationFunctionType
 ADD = mybir.AluOpType.add
 
 P = 128
+PACK = 4
 HALF = 512
+HALVES = ((0, HALF), (HALF, HALF))
+
 X_LOADS = (
-    (0, 0, 2048, (1408, 640, 0)),
-    (1, 0, 1024, (0, 0, 1024)),
-    (1, 1024, 1024, (0, 512, 512)),
-    (2, 0, 1024, (0, 0, 1024)),
-    (2, 1024, 1024, (0, 512, 512)),
-    (3, 0, 1024, (0, 0, 1024)),
-    (3, 1024, 1024, (0, 512, 512)),
+    (0, 0, (1408, 640, 0)),
+    (1, 0, (0, 0, 1024)),
+    (1, 1024, (0, 512, 512)),
+    (2, 0, (0, 0, 1024)),
+    (2, 1024, (0, 512, 512)),
+    (3, 0, (0, 0, 1024)),
+    (3, 1024, (0, 512, 512)),
 )
 VECTOR_ENTRIES = (640, 640, 512, 512)
 NODE_PIECES = ((0, 512), (512, 256), (768, 256))
-EDGE_PIECES = ((0, 256), (256, 256), (512, 256), (768, 128), (896, 128))
+QUARTER = 256
+WIDE = 1376
+EDGE_PIECES = ((0, 512), (512, 256), (768, 128), (896, 128))
+LAST = len(EDGE_PIECES) - 1
+
+KIB = 1024
+AT = {
+    "w2_woven0": 0,
+    "x_codes1": 0,
+    "w1_woven0": 2 * KIB,
+    "w2_codes0": 3 * KIB + KIB // 2,
+    "w1_woven2": 4 * KIB,
+    "sums1": 6 * KIB,
+    "e_picked3_0": 9 * KIB,
+    "sums2": 10 * KIB,
+    "z0": 12 * KIB,
+    "sums3": 12 * KIB,
+    "z1": 16 * KIB,
+    "z3": 16 * KIB,
+    "z2": 18 * KIB,
+    "z_codes3": 18 * KIB,
+}
 
 
 def tile_picked_hub_relu_e_kernel(tc, xT, w1, w2, w3_words, w3_scales, offs, src, dst, out):
@@ -39,29 +63,38 @@ def tile_picked_hub_relu_e_kernel(tc, xT, w1, w2, w3_words, w3_scales, offs, src
         shared = ctx.enter_context(tc.tile_pool(name="shared", bufs=1))
         psum = ctx.enter_context(tc.psum_pool(name="psum", bufs=1))
 
+        def new_tile(shape, dtype, name):
+            if name in AT:
+                return shared.tile(shape, dtype, name=name, align_bytes=64, offset=AT[name])
+            return keep.tile(shape, dtype, name=name, align_bytes=64)
+
         offs_sb = keep.tile([P, S // 16], U16, name="offs_sb")
         src_sb = keep.tile([P, S // 16], U16, name="src_sb")
         dst_sb = keep.tile([P, S // 16], U16, name="dst_sb")
 
-        w3_bytes = keep.tile([P, N], U8, name="w3_bytes", align_bytes=64)
-        w3_codes = keep.tile([P, 2 * N], U8, name="w3_codes", align_bytes=64)
+        def entries(lst, first, count):
+            return lst[:, first // 16 : (first + count) // 16]
+
+        w3_bytes = new_tile([P, N], U8, "w3_bytes")
+        w3_codes = new_tile([P, 2 * N], U8, "w3_codes")
         nc.vector.memset(w3_bytes[:].bitcast(I32), 0)
 
-        x_rows = xT.rearrange("(p j) t -> p j t", j=4)
-        x_raw = [keep.tile([P, T], F32, name=f"x_raw{j}") for j in range(4)]
-        for i, (j, c0, width, vec) in enumerate(X_LOADS):
-            nc.sync.dma_start(out=x_raw[j][:, c0 : c0 + width], in_=x_rows[:, j, c0 : c0 + width])
+        x_rows = xT.rearrange("(p j) t -> p j t", j=PACK)
+        x_raw = [new_tile([P, T], F32, f"x_raw{j}") for j in range(PACK)]
+        for i, (j, first, shares) in enumerate(X_LOADS):
+            nodes = slice(first, first + sum(shares))
+            nc.sync.dma_start(out=x_raw[j][:, nodes], in_=x_rows[:, j, nodes])
             if i == 0:
                 nc.sync.dma_start(offs_sb[:], offs)
 
         def load_w(w, name):
-            raw = keep.tile([P, 4, H], F32, name=f"{name}_raw")
-            nc.sync.dma_start(out=raw[:], in_=w.rearrange("(p j) c -> p j c", j=4))
+            raw = new_tile([P, PACK, H], F32, name)
+            nc.sync.dma_start(out=raw[:], in_=w.rearrange("(p j) c -> p j c", j=PACK))
             return raw
 
-        w2_raw = load_w(w2, "w2")
+        w2_raw = load_w(w2, "w2_raw")
         nc.sync.dma_start(dst_sb[:], dst)
-        w1_raw = load_w(w1, "w1")
+        w1_raw = load_w(w1, "w1_raw")
         nc.sync.dma_start(src_sb[:], src)
         nc.sync.dma_start(out=w3_codes[:].bitcast(I32), in_=w3_words[0].bitcast(I32))
         for q in range(4):
@@ -70,162 +103,151 @@ def tile_picked_hub_relu_e_kernel(tc, xT, w1, w2, w3_words, w3_scales, offs, src
                 in_=w3_scales[0, 4 * q : 4 * q + 4, :].bitcast(I32),
             )
 
-        x_half = [keep.tile([P, T], BF16, name=f"x_half{j}") for j in range(4)]
-        x_picked = keep.tile([P, 4 * S], BF16, name="x_picked", align_bytes=64)
-        x_codes = []
-        x_scales = keep.tile([P, S], U8, name="x_scales", align_bytes=64)
-
-        def cast_x(i):
-            j, c0, width, shares = X_LOADS[i]
-            for count, copy in zip(shares, (nc.vector.tensor_copy, nc.scalar.copy, nc.gpsimd.tensor_copy)):
-                if count:
-                    copy(out=x_half[j][:, c0 : c0 + count], in_=x_raw[j][:, c0 : c0 + count])
-                c0 += count
-
-        def entries(lst, first, count):
-            return lst[:, first // 16 : (first + count) // 16]
-
-        def gather_x(j, pieces):
-            planes = x_picked[:].rearrange("p (n j) -> p n j", j=4)
-            mine = VECTOR_ENTRIES[j]
-            nc.vector.tensor_copy(out=planes[:, 0:mine, j], in_=x_raw[j][:].indirect(entries(offs_sb, 0, mine)))
-            for n0, width in pieces:
-                nc.scalar.activation(
-                    out=planes[:, n0 : n0 + width, j], in_=x_half[j][:].indirect(entries(offs_sb, n0, width)), func=ACT.Copy
+        x_rounded = [new_tile([P, T], BF16, f"x_rounded{j}") for j in range(PACK)]
+        x_picked = new_tile([P, PACK * S], BF16, "x_picked")
+        picked_rows = x_picked[:].rearrange("p (n j) -> p n j", j=PACK)
+        for j in range(PACK):
+            for row, first, shares in X_LOADS:
+                if row == j:
+                    for count, copy in zip(shares, (nc.vector.tensor_copy, nc.scalar.copy, nc.gpsimd.tensor_copy)):
+                        if count:
+                            copy(out=x_rounded[j][:, first : first + count], in_=x_raw[j][:, first : first + count])
+                        first = first + count
+            split = VECTOR_ENTRIES[j]
+            step = QUARTER if j == PACK - 1 else split
+            for first in range(0, split, step):
+                nc.vector.tensor_copy(
+                    out=picked_rows[:, first : first + step, j], in_=x_raw[j][:].indirect(entries(offs_sb, first, step))
                 )
+            nc.scalar.activation(
+                out=picked_rows[:, split:S, j], in_=x_rounded[j][:].indirect(entries(offs_sb, split, S - split)), func=ACT.Copy
+            )
 
-        def x_words(n0, width):
-            return x_codes[n0 // HALF][:, n0 % HALF : n0 % HALF + width].bitcast(FP8X4)
+        x_codes = []
+        x_scales = new_tile([P, S], U8, "x_scales")
 
-        def quantize_x(i):
-            n0, width = NODE_PIECES[i]
-            nc.vector.quantize_mx(out=x_words(n0, width), scales=x_scales[:, n0 : n0 + width], in_=x_picked[:, 4 * n0 : 4 * (n0 + width)])
+        def x_words(first, count):
+            return x_codes[first // HALF][:, first % HALF : first % HALF + count].bitcast(FP8X4)
 
-        def tile_at(shape, dtype, name, offset):
-            if offset is None:
-                return keep.tile(shape, dtype, name=name, tag=name, align_bytes=64)
-            return shared.tile(shape, dtype, name=name, align_bytes=64, offset=offset)
+        def quantize_x(first, count):
+            if first % HALF == 0:
+                x_codes.append(new_tile([P, HALF], U32, f"x_codes{first // HALF}"))
+            nc.vector.quantize_mx(
+                out=x_words(first, count),
+                scales=x_scales[:, first : first + count],
+                in_=x_picked[:, PACK * first : PACK * (first + count)],
+            )
 
-        def quantize(values, width, name, offset=None):
-            codes = tile_at([P, width], U32, f"{name}_codes", offset)
-            scales = keep.tile([P, width], U8, name=f"{name}_scales", align_bytes=64)
-            nc.vector.quantize_mx(out=codes[:].bitcast(FP8X4), scales=scales[:], in_=values)
+        def quantize(values, columns, name, index):
+            codes = new_tile([P, columns], U32, f"{name}_codes{index}")
+            scales = new_tile([P, columns], U8, f"{name}_scales{index}")
+            nc.vector.quantize_mx(out=codes[:].bitcast(FP8X4), scales=scales[:], in_=values[:])
             return codes, scales
 
-        def weave_w(copy, raw, first, count, name, offset=None):
-            grouped = tile_at([P, count * H], BF16, f"{name}_grouped{first}", offset)
+        def weave_w(copy, raw, name, first):
+            woven = new_tile([P, 2 * H], BF16, f"{name}_woven{first}")
             copy(
-                out=grouped[:].rearrange("p (t m j) -> p m j t", t=count, j=4),
-                in_=raw[:].rearrange("p j (m t) -> p m j t", t=4)[:, :, :, first : first + count],
+                out=woven[:].rearrange("p (t m j) -> p m j t", t=2, j=PACK),
+                in_=raw[:].rearrange("p j (m t) -> p m j t", t=PACK)[:, :, :, first : first + 2],
             )
-            return grouped
+            return woven
 
-        def quantize_w(grouped, count, name, offset=None):
-            codes, scales = quantize(grouped, count * P, name, offset)
-            return [(codes[:, t * P : (t + 1) * P], scales[:, t * P : (t + 1) * P]) for t in range(count)]
+        def quantize_w(woven, name, first):
+            codes, scales = quantize(woven, 2 * P, name, first)
+            return [(codes[:, t * P : (t + 1) * P], scales[:, t * P : (t + 1) * P]) for t in range(2)]
 
         banks = [psum.tile([P, HALF], F32, name=f"bank{b}") for b in range(8)]
 
-        def product(w_q, t, name, pieces, where, by_vector=()):
-            rows = keep.tile([P, S], F32, name=f"{name}{t}")
-            codes, scales = w_q[t]
-            for i, (n0, width) in enumerate(pieces):
-                bank = banks[where[i]][:, 0:width]
+        def product(weights, plane, pieces, where, first_copy=nc.scalar.copy):
+            codes, scales = weights
+            for i, (first, count) in enumerate(pieces):
+                bank = banks[where[i]][:, 0:count]
                 nc.tensor.matmul_mx(
                     out=bank,
                     lhsT=codes.bitcast(FP8X4),
                     lhsT_scale=scales,
-                    rhs=x_words(n0, width),
-                    rhs_scale=x_scales[:, n0 : n0 + width],
+                    rhs=x_words(first, count),
+                    rhs_scale=x_scales[:, first : first + count],
                     start=True,
                     stop=True,
                 )
-                if i in by_vector:
-                    nc.vector.tensor_copy(out=rows[:, n0 : n0 + width], in_=bank)
-                else:
-                    nc.scalar.copy(out=rows[:, n0 : n0 + width], in_=bank)
-            return rows
+                copy = first_copy if i == 0 else nc.scalar.copy
+                copy(out=plane[:, first : first + count], in_=bank)
 
-        halves = ((0, HALF), (HALF, HALF))
+        quantize_x(0, QUARTER)
+        quantize_x(QUARTER, QUARTER)
+        w2_woven = [weave_w(nc.vector.tensor_copy, w2_raw, "w2", 0), weave_w(nc.scalar.copy, w2_raw, "w2", 2)]
+        w2_planes = quantize_w(w2_woven[0], "w2", 0)
+        for piece in NODE_PIECES[1:]:
+            quantize_x(*piece)
 
-        for j in range(4):
-            for i in range(len(X_LOADS)):
-                if X_LOADS[i][0] == j:
-                    cast_x(i)
-            gather_x(j, ((VECTOR_ENTRIES[j], S - VECTOR_ENTRIES[j]),))
-        x_codes.append(keep.tile([P, HALF], U32, name="x_codes0", align_bytes=64))
-        quantize_x(0)
-        w2_first = weave_w(nc.vector.tensor_copy, w2_raw, 0, 2, "w2")
-        w2_rest = weave_w(nc.scalar.copy, w2_raw, 2, 2, "w2")
-        w2_q = quantize_w(w2_first[:], 2, "w2a", offset=8192 + 1536)
-        x_codes.append(keep.tile([P, HALF], U32, name="x_codes1", tag="w2_grouped0", align_bytes=64))
-        quantize_x(1)
-        quantize_x(2)
+        e_all = new_tile([P, PACK * S], F32, "e_all")
+        e = [e_all[:, (PACK - 1 - t) * S : (PACK - t) * S] for t in range(PACK)]
+        product(w2_planes[0], e[0], NODE_PIECES, (0, 1, 2), first_copy=nc.vector.tensor_copy)
+        w2_planes += quantize_w(w2_woven[1], "w2", 2)
+        product(w2_planes[1], e[1], HALVES, (0, 3))
+        w1_woven = [weave_w(nc.scalar.copy, w1_raw, "w1", 0)]
+        product(w2_planes[2], e[2], HALVES, (4, 5))
+        w1_woven.append(weave_w(nc.scalar.copy, w1_raw, "w1", 2))
+        product(w2_planes[3], e[3], HALVES, (6, 7))
 
-        e_picked = {}
+        e_picked = []
 
-        def gather_e(rows, t, r0, width, tag=None):
-            picked = keep.tile([P, width], F32, name=f"e_picked{t}_{r0}", tag=tag or f"e_picked{t}_{r0}", align_bytes=64)
-            nc.vector.tensor_copy(out=picked[:], in_=rows[:].indirect(entries(dst_sb, r0, width)))
-            for r in range(r0, r0 + width, P):
-                e_picked[t, r] = (picked, r - r0)
+        def gather_e(t):
+            if t in (1, 2):
+                picked = new_tile([P, S], F32, f"e_picked{t}")
+                start = (PACK - 1 - t) * S
+                nc.vector.tensor_copy(out=picked[:], in_=e_all[:, start : start + WIDE].indirect(dst_sb[:]))
+                e_picked.append([picked[:, 0:HALF], picked[:, HALF:S]])
+                return
+            halves = []
+            for first, count in HALVES:
+                picked = new_tile([P, count], F32, f"e_picked{t}_{first}")
+                nc.vector.tensor_copy(out=picked[:], in_=e[t].indirect(entries(dst_sb, first, count)))
+                halves.append(picked)
+            e_picked.append(halves)
 
-        e_rows = [product(w2_q, 0, "e", NODE_PIECES, (0, 1, 2), by_vector=(0,))]
-        w2_q += quantize_w(w2_rest[:], 2, "w2b")
-        e_rows.append(product(w2_q, 1, "e", halves, (0, 3)))
-        w1_grouped = [weave_w(nc.scalar.copy, w1_raw, 0, 2, "w1", offset=8192)]
-        e_rows.append(product(w2_q, 2, "e", halves, (4, 5)))
-        w1_grouped.append(weave_w(nc.scalar.copy, w1_raw, 2, 2, "w1", offset=8192 + 2048))
-        e_rows.append(product(w2_q, 3, "e", halves, (6, 7)))
-        for t in range(2):
-            for r0, width in halves:
-                gather_e(e_rows[t], t, r0, width)
-        w1_q = quantize_w(w1_grouped[0][:], 2, "w1a")
-        for r0, width in halves:
-            gather_e(e_rows[2], 2, r0, width)
-        w1_q += quantize_w(w1_grouped[1][:], 2, "w1b")
-        gather_e(e_rows[3], 3, 0, 256, tag="sums1")
-        gather_e(e_rows[3], 3, 256, 768)
-        y_rows = [product(w1_q, t, "y", halves, (2 * t, 2 * t + 1)) for t in range(4)]
+        gather_e(0)
+        gather_e(1)
+        w1_planes = quantize_w(w1_woven[0], "w1", 0)
+        gather_e(2)
+        w1_planes += quantize_w(w1_woven[1], "w1", 2)
+        gather_e(3)
+        y = [new_tile([P, S], F32, f"y{t}") for t in range(PACK)]
+        for t in range(PACK):
+            product(w1_planes[t], y[t], HALVES, (2 * t, 2 * t + 1))
 
-        places = {1: 0, 2: 2048, 4: 2048, 3: 4096}
-        z = [
-            shared.tile([P, 4 * width], BF16, name=f"z{c}", align_bytes=64, offset=places[c])
-            if c in places
-            else keep.tile([P, 4 * width], BF16, name=f"z{c}", align_bytes=64)
-            for c, (r0, width) in enumerate(EDGE_PIECES)
-        ]
+        sums = []
+        z = []
 
-        def gather_y(sums, t, r0, width):
-            picked, at = e_picked[t, r0]
-            nc.vector.tensor_tensor(
-                out=sums, in0=y_rows[t][:].indirect(entries(src_sb, r0, width)), in1=picked[:, at : at + width], op=ADD
-            )
-
-        all_sums = []
-
-        def edges(c):
-            r0, width = EDGE_PIECES[c]
-            if c == len(EDGE_PIECES) - 1:
-                sums = shared.tile([P, 4, width], F32, name="sums_last", align_bytes=64, offset=0)
-            else:
-                sums = keep.tile([P, 4, width], F32, name=f"sums{c}", tag=f"sums{c % 2}", align_bytes=64)
-            all_sums.append(sums)
-            for t in range(4):
-                gather_y(sums[:, t, :], t, r0, width)
+        def gather_y(c):
+            first, count = EDGE_PIECES[c]
+            sums.append(new_tile([P, PACK, count], F32, f"sums{c}"))
+            for t in range(PACK):
+                nc.vector.tensor_tensor(
+                    out=sums[c][:, t, :],
+                    in0=y[t][:].indirect(entries(src_sb, first, count)),
+                    in1=e_picked[t][first // HALF][:, first % HALF : first % HALF + count],
+                    op=ADD,
+                )
 
         def relu(c):
-            rounded = z[c][:].rearrange("p (c i t) -> p c t i", i=4, t=4)
-            planes = all_sums[c][:].rearrange("p t (c i) -> p c t i", i=4)
-            if c == len(EDGE_PIECES) - 1:
-                nc.vector.tensor_scalar_max(out=z[c][:].rearrange("p (n t) -> p n t", t=4), in0=all_sums[c][:].rearrange("p t n -> p n t"), scalar1=0.0)
+            z.append(new_tile([P, PACK * EDGE_PIECES[c][1]], BF16, f"z{c}"))
+            if c == LAST:
+                nc.vector.tensor_scalar_max(
+                    out=z[c][:].rearrange("p (n t) -> p n t", t=PACK), in0=sums[c][:].rearrange("p t n -> p n t"), scalar1=0.0
+                )
             else:
-                nc.scalar.activation(out=rounded, in_=planes, func=ACT.Relu)
+                nc.scalar.activation(
+                    out=z[c][:].rearrange("p (g i t) -> p g t i", i=4, t=PACK),
+                    in_=sums[c][:].rearrange("p t (g i) -> p g t i", i=4),
+                    func=ACT.Relu,
+                )
 
         def finish(c):
-            r0, width = EDGE_PIECES[c]
-            codes, scales = quantize(z[c][:], width, f"z{c}", places[3] if c == len(EDGE_PIECES) - 1 else None)
-            bank = banks[c][:, 0:width]
+            first, count = EDGE_PIECES[c]
+            codes, scales = quantize(z[c], count, "z", c)
+            bank = banks[c][:, 0:count]
             nc.tensor.matmul_mx(
                 out=bank,
                 lhsT=w3_codes[:].bitcast(FP4X4),
@@ -235,25 +257,17 @@ def tile_picked_hub_relu_e_kernel(tc, xT, w1, w2, w3_words, w3_scales, offs, src
                 start=True,
                 stop=True,
             )
-            result = keep.tile([P, width], F32, name=f"result{c}")
-            if c == len(EDGE_PIECES) - 1:
-                nc.vector.tensor_copy(out=result[:], in_=bank)
-            else:
-                nc.scalar.copy(out=result[:], in_=bank)
-            nc.sync.dma_start(out=out[:, r0 : r0 + width], in_=result[:])
+            result = new_tile([P, count], F32, f"result{c}")
+            copy = nc.vector.tensor_copy if c == LAST else nc.scalar.copy
+            copy(out=result[:], in_=bank)
+            nc.sync.dma_start(out=out[:, first : first + count], in_=result[:])
 
-        edges(0)
-        relu(0)
-        edges(1)
-        relu(1)
+        for c in range(LAST):
+            gather_y(c)
+            relu(c)
         finish(0)
-        edges(2)
-        relu(2)
+        gather_y(LAST)
         finish(1)
-        edges(3)
-        relu(3)
-        edges(4)
+        relu(LAST)
         finish(2)
-        relu(4)
-        finish(len(EDGE_PIECES) - 2)
-        finish(len(EDGE_PIECES) - 1)
+        finish(LAST)

@@ -35,6 +35,7 @@ NODE_PIECES = ((0, 512), (512, 256), (768, 256))
 QUARTER = 256
 WIDE = 1376
 EDGE_PIECES = ((0, 512), (512, 256), (768, 128), (896, 128))
+GATHER_PIECES = ((0, 512), (512, 384), (896, 128))
 LAST = len(EDGE_PIECES) - 1
 
 KIB = 1024
@@ -45,10 +46,9 @@ AT = {
     "w2_codes0": 3 * KIB + KIB // 2,
     "w1_woven2": 4 * KIB,
     "sums1": 6 * KIB,
-    "e_picked3_0": 9 * KIB,
-    "sums2": 10 * KIB,
+    "e_picked3_0": 6 * KIB,
     "z0": 12 * KIB,
-    "sums3": 12 * KIB,
+    "sums2": 12 * KIB,
     "z1": 16 * KIB,
     "z3": 16 * KIB,
     "z2": 18 * KIB,
@@ -181,7 +181,7 @@ def tile_picked_hub_relu_e_kernel(tc, xT, w1, w2, w3_words, w3_scales, offs, src
         for piece in NODE_PIECES[1:]:
             quantize_x(*piece)
 
-        e_all = new_tile([P, PACK * S], F32, "e_all")
+        e_all = new_tile([P, (PACK - 1) * S + WIDE], F32, "e_all")
         e = [e_all[:, (PACK - 1 - t) * S : (PACK - t) * S] for t in range(PACK)]
         product(w2_planes[0], e[0], NODE_PIECES, (0, 1, 2), first_copy=nc.vector.tensor_copy)
         w2_planes += quantize_w(w2_woven[1], "w2", 2)
@@ -194,7 +194,7 @@ def tile_picked_hub_relu_e_kernel(tc, xT, w1, w2, w3_words, w3_scales, offs, src
         e_picked = []
 
         def gather_e(t):
-            if t in (1, 2):
+            if t < PACK - 1:
                 picked = new_tile([P, S], F32, f"e_picked{t}")
                 start = (PACK - 1 - t) * S
                 nc.vector.tensor_copy(out=picked[:], in_=e_all[:, start : start + WIDE].indirect(dst_sb[:]))
@@ -220,27 +220,30 @@ def tile_picked_hub_relu_e_kernel(tc, xT, w1, w2, w3_words, w3_scales, offs, src
         sums = []
         z = []
 
-        def gather_y(c):
-            first, count = EDGE_PIECES[c]
-            sums.append(new_tile([P, PACK, count], F32, f"sums{c}"))
+        def gather_y(g):
+            first, count = GATHER_PIECES[g]
+            sums.append(new_tile([P, PACK, count], F32, f"sums{g}"))
             for t in range(PACK):
                 nc.vector.tensor_tensor(
-                    out=sums[c][:, t, :],
+                    out=sums[g][:, t, :],
                     in0=y[t][:].indirect(entries(src_sb, first, count)),
                     in1=e_picked[t][first // HALF][:, first % HALF : first % HALF + count],
                     op=ADD,
                 )
 
-        def relu(c):
-            z.append(new_tile([P, PACK * EDGE_PIECES[c][1]], BF16, f"z{c}"))
+        def relu(c, g):
+            first, count = EDGE_PIECES[c]
+            at = first - GATHER_PIECES[g][0]
+            values = sums[g][:, :, at : at + count]
+            z.append(new_tile([P, PACK * count], BF16, f"z{c}"))
             if c == LAST:
                 nc.vector.tensor_scalar_max(
-                    out=z[c][:].rearrange("p (n t) -> p n t", t=PACK), in0=sums[c][:].rearrange("p t n -> p n t"), scalar1=0.0
+                    out=z[c][:].rearrange("p (n t) -> p n t", t=PACK), in0=values.rearrange("p t n -> p n t"), scalar1=0.0
                 )
             else:
                 nc.scalar.activation(
                     out=z[c][:].rearrange("p (g i t) -> p g t i", i=4, t=PACK),
-                    in_=sums[c][:].rearrange("p t (g i) -> p g t i", i=4),
+                    in_=values.rearrange("p t (g i) -> p g t i", i=4),
                     func=ACT.Relu,
                 )
 
@@ -262,12 +265,14 @@ def tile_picked_hub_relu_e_kernel(tc, xT, w1, w2, w3_words, w3_scales, offs, src
             copy(out=result[:], in_=bank)
             nc.sync.dma_start(out=out[:, first : first + count], in_=result[:])
 
-        for c in range(LAST):
-            gather_y(c)
-            relu(c)
+        gather_y(0)
+        relu(0, 0)
+        gather_y(1)
+        relu(1, 1)
+        relu(2, 1)
         finish(0)
-        gather_y(LAST)
+        gather_y(2)
         finish(1)
-        relu(LAST)
+        relu(LAST, 2)
         finish(2)
         finish(LAST)

@@ -31,11 +31,12 @@ X_LOADS = (
     (3, 1024, (0, 512, 512)),
 )
 VECTOR_ENTRIES = (640, 640, 512, 512)
-NODE_PIECES = ((0, 512), (512, 256), (768, 256))
+NODE_PIECES = ((0, 256), (256, 256), (512, 256), (768, 128), (896, 128))
+LATE_NODES = ((512, 256), (768, 256))
 QUARTER = 256
 WIDE = 1376
 EDGE_PIECES = ((0, 512), (512, 256), (768, 128), (896, 128))
-GATHER_PIECES = ((0, 512), (512, 384), (896, 128))
+EARLY = 896
 LAST = len(EDGE_PIECES) - 1
 
 KIB = 1024
@@ -45,14 +46,13 @@ AT = {
     "w1_woven0": 2 * KIB,
     "w2_codes0": 3 * KIB + KIB // 2,
     "w1_woven2": 4 * KIB,
-    "sums1": 6 * KIB,
-    "e_picked3_0": 6 * KIB,
-    "z0": 12 * KIB,
-    "sums2": 12 * KIB,
-    "z1": 16 * KIB,
-    "z3": 16 * KIB,
-    "z2": 18 * KIB,
-    "z_codes3": 18 * KIB,
+    "sums0": 0,
+    "z0": 14 * KIB,
+    "sums1": 14 * KIB,
+    "z1": 18 * KIB,
+    "z3": 18 * KIB,
+    "z2": 20 * KIB,
+    "z_codes3": 20 * KIB,
 }
 
 
@@ -158,7 +158,7 @@ def tile_picked_hub_relu_e_kernel(tc, xT, w1, w2, w3_words, w3_scales, offs, src
 
         banks = [psum.tile([P, HALF], F32, name=f"bank{b}") for b in range(8)]
 
-        def product(weights, plane, pieces, where, first_copy=nc.scalar.copy):
+        def product(weights, plane, pieces, where, by_vector=()):
             codes, scales = weights
             for i, (first, count) in enumerate(pieces):
                 bank = banks[where[i]][:, 0:count]
@@ -171,41 +171,33 @@ def tile_picked_hub_relu_e_kernel(tc, xT, w1, w2, w3_words, w3_scales, offs, src
                     start=True,
                     stop=True,
                 )
-                copy = first_copy if i == 0 else nc.scalar.copy
+                copy = nc.vector.tensor_copy if i in by_vector else nc.scalar.copy
                 copy(out=plane[:, first : first + count], in_=bank)
 
         quantize_x(0, QUARTER)
         quantize_x(QUARTER, QUARTER)
         w2_woven = [weave_w(nc.vector.tensor_copy, w2_raw, "w2", 0), weave_w(nc.scalar.copy, w2_raw, "w2", 2)]
         w2_planes = quantize_w(w2_woven[0], "w2", 0)
-        for piece in NODE_PIECES[1:]:
+        for piece in LATE_NODES:
             quantize_x(*piece)
 
         e_all = new_tile([P, (PACK - 1) * S + WIDE], F32, "e_all")
         e = [e_all[:, (PACK - 1 - t) * S : (PACK - t) * S] for t in range(PACK)]
-        product(w2_planes[0], e[0], NODE_PIECES, (0, 1, 2), first_copy=nc.vector.tensor_copy)
+        product(w2_planes[0], e[0], NODE_PIECES, (0, 1, 2, 3, 4), by_vector=(0, 2))
         w2_planes += quantize_w(w2_woven[1], "w2", 2)
-        product(w2_planes[1], e[1], HALVES, (0, 3))
+        product(w2_planes[1], e[1], HALVES, (3, 4))
         w1_woven = [weave_w(nc.scalar.copy, w1_raw, "w1", 0)]
-        product(w2_planes[2], e[2], HALVES, (4, 5))
+        product(w2_planes[2], e[2], HALVES, (5, 6))
         w1_woven.append(weave_w(nc.scalar.copy, w1_raw, "w1", 2))
-        product(w2_planes[3], e[3], HALVES, (6, 7))
+        product(w2_planes[3], e[3], HALVES, (7, 0))
 
         e_picked = []
 
         def gather_e(t):
-            if t < PACK - 1:
-                picked = new_tile([P, S], F32, f"e_picked{t}")
-                start = (PACK - 1 - t) * S
-                nc.vector.tensor_copy(out=picked[:], in_=e_all[:, start : start + WIDE].indirect(dst_sb[:]))
-                e_picked.append([picked[:, 0:HALF], picked[:, HALF:S]])
-                return
-            halves = []
-            for first, count in HALVES:
-                picked = new_tile([P, count], F32, f"e_picked{t}_{first}")
-                nc.vector.tensor_copy(out=picked[:], in_=e[t].indirect(entries(dst_sb, first, count)))
-                halves.append(picked)
-            e_picked.append(halves)
+            picked = new_tile([P, S], F32, f"e_picked{t}")
+            start = (PACK - 1 - t) * S
+            nc.vector.tensor_copy(out=picked[:], in_=e_all[:, start : start + WIDE].indirect(dst_sb[:]))
+            e_picked.append(picked)
 
         gather_e(0)
         gather_e(1)
@@ -214,27 +206,25 @@ def tile_picked_hub_relu_e_kernel(tc, xT, w1, w2, w3_words, w3_scales, offs, src
         w1_planes += quantize_w(w1_woven[1], "w1", 2)
         gather_e(3)
         y = [new_tile([P, S], F32, f"y{t}") for t in range(PACK)]
-        for t in range(PACK):
-            product(w1_planes[t], y[t], HALVES, (2 * t, 2 * t + 1))
+        for t, where in enumerate(((1, 2), (3, 4), (5, 6), (3, 4))):
+            product(w1_planes[t], y[t], HALVES, where)
 
-        sums = []
+        sums = [new_tile([P, PACK, EARLY], F32, "sums0")]
         z = []
 
-        def gather_y(g):
-            first, count = GATHER_PIECES[g]
-            sums.append(new_tile([P, PACK, count], F32, f"sums{g}"))
-            for t in range(PACK):
-                nc.vector.tensor_tensor(
-                    out=sums[g][:, t, :],
-                    in0=y[t][:].indirect(entries(src_sb, first, count)),
-                    in1=e_picked[t][first // HALF][:, first % HALF : first % HALF + count],
-                    op=ADD,
-                )
+        def gather_y(t, first, count):
+            at = first % EARLY
+            nc.vector.tensor_tensor(
+                out=sums[first // EARLY][:, t, at : at + count],
+                in0=y[t][:].indirect(entries(src_sb, first, count)),
+                in1=e_picked[t][:, first : first + count],
+                op=ADD,
+            )
 
-        def relu(c, g):
+        def relu(c):
             first, count = EDGE_PIECES[c]
-            at = first - GATHER_PIECES[g][0]
-            values = sums[g][:, :, at : at + count]
+            at = first % EARLY
+            values = sums[first // EARLY][:, :, at : at + count]
             z.append(new_tile([P, PACK * count], BF16, f"z{c}"))
             if c == LAST:
                 nc.vector.tensor_scalar_max(
@@ -265,14 +255,19 @@ def tile_picked_hub_relu_e_kernel(tc, xT, w1, w2, w3_words, w3_scales, offs, src
             copy(out=result[:], in_=bank)
             nc.sync.dma_start(out=out[:, first : first + count], in_=result[:])
 
-        gather_y(0)
-        relu(0, 0)
-        gather_y(1)
-        relu(1, 1)
-        relu(2, 1)
+        gather_y(0, 0, EARLY)
+        for t in range(1, PACK):
+            gather_y(t, 0, HALF)
+        relu(0)
+        for t in range(1, PACK):
+            gather_y(t, HALF, EARLY - HALF)
+        relu(1)
+        relu(2)
         finish(0)
-        gather_y(2)
+        sums.append(new_tile([P, PACK, S - EARLY], F32, "sums1"))
+        for t in range(PACK):
+            gather_y(t, EARLY, S - EARLY)
         finish(1)
-        relu(LAST, 2)
+        relu(LAST)
         finish(2)
         finish(LAST)

@@ -35,8 +35,11 @@ NODE_PIECES = ((0, 256), (256, 256), (512, 256), (768, 128), (896, 128))
 LATE_NODES = ((512, 256), (768, 256))
 QUARTER = 256
 WIDE = 1376
-EDGE_PIECES = ((0, 512), (512, 256), (768, 128), (896, 128))
-EARLY = 896
+EDGE_PIECES = ((512, 512), (256, 256), (128, 128), (0, 128))
+LATE = 128
+MIDDLE = HALF - LATE
+UPPER_STEP = 2560
+MIDDLE_AT = 3 * UPPER_STEP - PACK * MIDDLE
 LAST = len(EDGE_PIECES) - 1
 
 KIB = 1024
@@ -46,13 +49,6 @@ AT = {
     "w1_woven0": 2 * KIB,
     "w2_codes0": 3 * KIB + KIB // 2,
     "w1_woven2": 4 * KIB,
-    "sums0": 0,
-    "z0": 14 * KIB,
-    "sums1": 14 * KIB,
-    "z1": 18 * KIB,
-    "z3": 18 * KIB,
-    "z2": 20 * KIB,
-    "z_codes3": 20 * KIB,
 }
 
 
@@ -185,18 +181,22 @@ def tile_picked_hub_relu_e_kernel(tc, xT, w1, w2, w3_words, w3_scales, offs, src
         e = [e_all[:, (PACK - 1 - t) * S : (PACK - t) * S] for t in range(PACK)]
         product(w2_planes[0], e[0], NODE_PIECES, (0, 1, 2, 3, 4), by_vector=(0, 2))
         w2_planes += quantize_w(w2_woven[1], "w2", 2)
-        product(w2_planes[1], e[1], HALVES, (3, 4))
+        product(w2_planes[1], e[1], HALVES, (2, 5))
         w1_woven = [weave_w(nc.scalar.copy, w1_raw, "w1", 0)]
-        product(w2_planes[2], e[2], HALVES, (5, 6))
+        product(w2_planes[2], e[2], HALVES, (6, 7))
         w1_woven.append(weave_w(nc.scalar.copy, w1_raw, "w1", 2))
-        product(w2_planes[3], e[3], HALVES, (7, 0))
+        product(w2_planes[3], e[3], HALVES, (0, 1))
 
         e_picked = []
+        sums = new_tile([P, PACK * UPPER_STEP], F32, "sums")
 
         def gather_e(t):
-            picked = new_tile([P, S], F32, f"e_picked{t}")
+            if t == 2:
+                picked = sums[:, MIDDLE_AT - HALF : MIDDLE_AT + HALF]
+            else:
+                picked = new_tile([P, S], F32, f"e_picked{t}")[:]
             start = (PACK - 1 - t) * S
-            nc.vector.tensor_copy(out=picked[:], in_=e_all[:, start : start + WIDE].indirect(dst_sb[:]))
+            nc.vector.tensor_copy(out=picked, in_=e_all[:, start : start + WIDE].indirect(dst_sb[:]))
             e_picked.append(picked)
 
         gather_e(0)
@@ -206,25 +206,23 @@ def tile_picked_hub_relu_e_kernel(tc, xT, w1, w2, w3_words, w3_scales, offs, src
         w1_planes += quantize_w(w1_woven[1], "w1", 2)
         gather_e(3)
         y = [new_tile([P, S], F32, f"y{t}") for t in range(PACK)]
-        for t, where in enumerate(((1, 2), (3, 4), (5, 6), (3, 4))):
+        for t, where in ((0, (2, 3)), (1, (4, 5)), (3, (6, 7)), (2, (0, 1))):
             product(w1_planes[t], y[t], HALVES, where)
 
-        sums = [new_tile([P, PACK, EARLY], F32, "sums0")]
+        upper = sums[:].rearrange("p (t n) -> p t n", t=PACK)[:, :, 0:HALF]
+        middle = sums[:, MIDDLE_AT : MIDDLE_AT + PACK * MIDDLE].rearrange("p (t n) -> p t n", t=PACK)
         z = []
 
-        def gather_y(t, first, count):
-            at = first % EARLY
+        def gather_y(t, first, count, target):
             nc.vector.tensor_tensor(
-                out=sums[first // EARLY][:, t, at : at + count],
+                out=target,
                 in0=y[t][:].indirect(entries(src_sb, first, count)),
                 in1=e_picked[t][:, first : first + count],
                 op=ADD,
             )
 
-        def relu(c):
+        def relu(c, values):
             first, count = EDGE_PIECES[c]
-            at = first % EARLY
-            values = sums[first // EARLY][:, :, at : at + count]
             z.append(new_tile([P, PACK * count], BF16, f"z{c}"))
             if c == LAST:
                 nc.vector.tensor_scalar_max(
@@ -255,19 +253,20 @@ def tile_picked_hub_relu_e_kernel(tc, xT, w1, w2, w3_words, w3_scales, offs, src
             copy(out=result[:], in_=bank)
             nc.sync.dma_start(out=out[:, first : first + count], in_=result[:])
 
-        gather_y(0, 0, EARLY)
-        for t in range(1, PACK):
-            gather_y(t, 0, HALF)
-        relu(0)
-        for t in range(1, PACK):
-            gather_y(t, HALF, EARLY - HALF)
-        relu(1)
-        relu(2)
+        gather_y(0, HALF, HALF, upper[:, 0, :])
+        gather_y(1, HALF, HALF, upper[:, 1, :])
+        gather_y(3, LATE, S - LATE, sums[:, MIDDLE_AT + 3 * MIDDLE : 3 * UPPER_STEP + HALF])
+        gather_y(2, HALF, HALF, upper[:, 2, :])
+        relu(0, upper)
+        for t in (2, 0, 1):
+            gather_y(t, LATE, MIDDLE, middle[:, t, :])
+        relu(1, middle[:, :, LATE:MIDDLE])
+        relu(2, middle[:, :, 0:LATE])
         finish(0)
-        sums.append(new_tile([P, PACK, S - EARLY], F32, "sums1"))
+        late = upper[:, :, 0:LATE]
         for t in range(PACK):
-            gather_y(t, EARLY, S - EARLY)
+            gather_y(t, 0, LATE, late[:, t, :])
         finish(1)
-        relu(LAST)
+        relu(LAST, late)
         finish(2)
         finish(LAST)

@@ -44,11 +44,11 @@ LAST = len(EDGE_PIECES) - 1
 
 KIB = 1024
 AT = {
-    "w2_woven0": 0,
+    "w1_woven0": 0,
     "x_codes1": 0,
-    "w1_woven0": 2 * KIB,
-    "w2_codes0": 3 * KIB + KIB // 2,
-    "w1_woven2": 4 * KIB,
+    "w2_woven0": 2 * KIB,
+    "w1_codes0": 3 * KIB + KIB // 2,
+    "w2_woven2": 4 * KIB,
 }
 
 
@@ -65,8 +65,8 @@ def tile_picked_hub_relu_e_kernel(tc, xT, w1, w2, w3_words, w3_scales, offs, src
             return keep.tile(shape, dtype, name=name, align_bytes=64)
 
         offs_sb = keep.tile([P, S // 16], U16, name="offs_sb")
-        src_sb = keep.tile([P, S // 16], U16, name="src_sb")
         dst_sb = keep.tile([P, S // 16], U16, name="dst_sb")
+        src_sb = keep.tile([P, S // 16], U16, name="src_sb")
 
         def entries(lst, first, count):
             return lst[:, first // 16 : (first + count) // 16]
@@ -88,10 +88,10 @@ def tile_picked_hub_relu_e_kernel(tc, xT, w1, w2, w3_words, w3_scales, offs, src
             nc.sync.dma_start(out=raw[:], in_=w.rearrange("(p j) c -> p j c", j=PACK))
             return raw
 
-        w2_raw = load_w(w2, "w2_raw")
-        nc.sync.dma_start(dst_sb[:], dst)
         w1_raw = load_w(w1, "w1_raw")
         nc.sync.dma_start(src_sb[:], src)
+        w2_raw = load_w(w2, "w2_raw")
+        nc.sync.dma_start(dst_sb[:], dst)
         nc.sync.dma_start(out=w3_codes[:].bitcast(I32), in_=w3_words[0].bitcast(I32))
         for q in range(4):
             nc.sync.dma_start(
@@ -172,52 +172,52 @@ def tile_picked_hub_relu_e_kernel(tc, xT, w1, w2, w3_words, w3_scales, offs, src
 
         quantize_x(0, QUARTER)
         quantize_x(QUARTER, QUARTER)
-        w2_woven = [weave_w(nc.vector.tensor_copy, w2_raw, "w2", 0), weave_w(nc.scalar.copy, w2_raw, "w2", 2)]
-        w2_planes = quantize_w(w2_woven[0], "w2", 0)
+        w1_woven = [weave_w(nc.vector.tensor_copy, w1_raw, "w1", 0), weave_w(nc.scalar.copy, w1_raw, "w1", 2)]
+        w1_planes = quantize_w(w1_woven[0], "w1", 0)
         for piece in LATE_NODES:
             quantize_x(*piece)
 
-        e_all = new_tile([P, (PACK - 1) * S + WIDE], F32, "e_all")
-        e = [e_all[:, (PACK - 1 - t) * S : (PACK - t) * S] for t in range(PACK)]
-        product(w2_planes[0], e[0], NODE_PIECES, (0, 1, 2, 3, 4), by_vector=(0, 2))
-        w2_planes += quantize_w(w2_woven[1], "w2", 2)
-        product(w2_planes[1], e[1], HALVES, (2, 5))
-        w1_woven = [weave_w(nc.scalar.copy, w1_raw, "w1", 0)]
-        product(w2_planes[2], e[2], HALVES, (6, 7))
-        w1_woven.append(weave_w(nc.scalar.copy, w1_raw, "w1", 2))
-        product(w2_planes[3], e[3], HALVES, (0, 1))
+        y_all = new_tile([P, (PACK - 1) * S + WIDE], F32, "y_all")
+        y = [y_all[:, (PACK - 1 - t) * S : (PACK - t) * S] for t in range(PACK)]
+        product(w1_planes[0], y[0], NODE_PIECES, (0, 1, 2, 3, 4), by_vector=(0, 2))
+        w1_planes += quantize_w(w1_woven[1], "w1", 2)
+        product(w1_planes[1], y[1], HALVES, (2, 5))
+        w2_woven = [weave_w(nc.scalar.copy, w2_raw, "w2", 0)]
+        product(w1_planes[2], y[2], HALVES, (6, 7))
+        w2_woven.append(weave_w(nc.scalar.copy, w2_raw, "w2", 2))
+        product(w1_planes[3], y[3], HALVES, (0, 1))
 
-        e_picked = []
+        y_picked = []
         sums = new_tile([P, PACK * UPPER_STEP], F32, "sums")
 
-        def gather_e(t):
+        def gather_y(t):
             if t == 2:
                 picked = sums[:, MIDDLE_AT - HALF : MIDDLE_AT + HALF]
             else:
-                picked = new_tile([P, S], F32, f"e_picked{t}")[:]
+                picked = new_tile([P, S], F32, f"y_picked{t}")[:]
             start = (PACK - 1 - t) * S
-            nc.vector.tensor_copy(out=picked, in_=e_all[:, start : start + WIDE].indirect(dst_sb[:]))
-            e_picked.append(picked)
+            nc.vector.tensor_copy(out=picked, in_=y_all[:, start : start + WIDE].indirect(src_sb[:]))
+            y_picked.append(picked)
 
-        gather_e(0)
-        gather_e(1)
-        w1_planes = quantize_w(w1_woven[0], "w1", 0)
-        gather_e(2)
-        w1_planes += quantize_w(w1_woven[1], "w1", 2)
-        gather_e(3)
-        y = [new_tile([P, S], F32, f"y{t}") for t in range(PACK)]
+        gather_y(0)
+        gather_y(1)
+        w2_planes = quantize_w(w2_woven[0], "w2", 0)
+        gather_y(2)
+        w2_planes += quantize_w(w2_woven[1], "w2", 2)
+        gather_y(3)
+        e = [new_tile([P, S], F32, f"e{t}") for t in range(PACK)]
         for t, where in ((0, (2, 3)), (1, (4, 5)), (3, (6, 7)), (2, (0, 1))):
-            product(w1_planes[t], y[t], HALVES, where)
+            product(w2_planes[t], e[t], HALVES, where)
 
         upper = sums[:].rearrange("p (t n) -> p t n", t=PACK)[:, :, 0:HALF]
         middle = sums[:, MIDDLE_AT : MIDDLE_AT + PACK * MIDDLE].rearrange("p (t n) -> p t n", t=PACK)
         z = []
 
-        def gather_y(t, first, count, target):
+        def gather_e(t, first, count, target):
             nc.vector.tensor_tensor(
                 out=target,
-                in0=y[t][:].indirect(entries(src_sb, first, count)),
-                in1=e_picked[t][:, first : first + count],
+                in0=e[t][:].indirect(entries(dst_sb, first, count)),
+                in1=y_picked[t][:, first : first + count],
                 op=ADD,
             )
 
@@ -253,19 +253,19 @@ def tile_picked_hub_relu_e_kernel(tc, xT, w1, w2, w3_words, w3_scales, offs, src
             copy(out=result[:], in_=bank)
             nc.sync.dma_start(out=out[:, first : first + count], in_=result[:])
 
-        gather_y(0, HALF, HALF, upper[:, 0, :])
-        gather_y(1, HALF, HALF, upper[:, 1, :])
-        gather_y(3, LATE, S - LATE, sums[:, MIDDLE_AT + 3 * MIDDLE : 3 * UPPER_STEP + HALF])
-        gather_y(2, HALF, HALF, upper[:, 2, :])
+        gather_e(0, HALF, HALF, upper[:, 0, :])
+        gather_e(1, HALF, HALF, upper[:, 1, :])
+        gather_e(3, LATE, S - LATE, sums[:, MIDDLE_AT + 3 * MIDDLE : 3 * UPPER_STEP + HALF])
+        gather_e(2, HALF, HALF, upper[:, 2, :])
         relu(0, upper)
         for t in (2, 0, 1):
-            gather_y(t, LATE, MIDDLE, middle[:, t, :])
+            gather_e(t, LATE, MIDDLE, middle[:, t, :])
         relu(1, middle[:, :, LATE:MIDDLE])
         relu(2, middle[:, :, 0:LATE])
         finish(0)
         late = upper[:, :, 0:LATE]
         for t in range(PACK):
-            gather_y(t, 0, LATE, late[:, t, :])
+            gather_e(t, 0, LATE, late[:, t, :])
         finish(1)
         relu(LAST, late)
         finish(2)

@@ -23,23 +23,25 @@ HALVES = ((0, HALF), (HALF, HALF))
 
 X_LOADS = (
     (0, 0, (1408, 640, 0)),
-    (1, 0, (0, 0, 1024)),
-    (1, 1024, (0, 512, 512)),
     (2, 0, (0, 0, 1024)),
     (2, 1024, (0, 512, 512)),
+    (1, 0, (0, 0, 1024)),
+    (1, 1024, (0, 512, 512)),
     (3, 0, (0, 0, 1024)),
     (3, 1024, (0, 512, 512)),
 )
+ROW_ORDER = (0, 2, 1, 3)
 VECTOR_ENTRIES = (640, 640, 512, 512)
 NODE_PIECES = ((0, 256), (256, 256), (512, 256), (768, 128), (896, 128))
+SECOND_PIECES = ((768, 256), (512, 256), (0, 256), (256, 256))
 LATE_NODES = ((512, 256), (768, 256))
 QUARTER = 256
 WIDE = 1376
 EDGE_PIECES = ((512, 512), (256, 256), (128, 128), (0, 128))
 LATE = 128
 MIDDLE = HALF - LATE
-UPPER_STEP = 2560
-MIDDLE_AT = 3 * UPPER_STEP - PACK * MIDDLE
+PICKED_AT = PACK * HALF
+MIDDLE_AT = PICKED_AT + HALF + (HALF - MIDDLE) // 2 - MIDDLE
 LAST = len(EDGE_PIECES) - 1
 
 KIB = 1024
@@ -49,6 +51,8 @@ AT = {
     "w2_woven0": 2 * KIB,
     "w1_codes0": 3 * KIB + KIB // 2,
     "w2_woven2": 4 * KIB,
+    "x_picked": 6 * KIB,
+    "w1_codes2": 6 * KIB,
 }
 
 
@@ -102,7 +106,7 @@ def tile_picked_hub_relu_e_kernel(tc, xT, w1, w2, w3_words, w3_scales, offs, src
         x_rounded = [new_tile([P, T], BF16, f"x_rounded{j}") for j in range(PACK)]
         x_picked = new_tile([P, PACK * S], BF16, "x_picked")
         picked_rows = x_picked[:].rearrange("p (n j) -> p n j", j=PACK)
-        for j in range(PACK):
+        for j in ROW_ORDER:
             for row, first, shares in X_LOADS:
                 if row == j:
                     for count, copy in zip(shares, (nc.vector.tensor_copy, nc.scalar.copy, nc.gpsimd.tensor_copy)):
@@ -140,13 +144,14 @@ def tile_picked_hub_relu_e_kernel(tc, xT, w1, w2, w3_words, w3_scales, offs, src
             nc.vector.quantize_mx(out=codes[:].bitcast(FP8X4), scales=scales[:], in_=values[:])
             return codes, scales
 
-        def weave_w(copy, raw, name, first):
-            woven = new_tile([P, 2 * H], BF16, f"{name}_woven{first}")
+        def weave_w(copy, raw, woven, first, rows=slice(0, P)):
             copy(
-                out=woven[:].rearrange("p (t m j) -> p m j t", t=2, j=PACK),
-                in_=raw[:].rearrange("p j (m t) -> p m j t", t=PACK)[:, :, :, first : first + 2],
+                out=woven[:].rearrange("p (t m j) -> p m j t", t=2, j=PACK)[:, rows],
+                in_=raw[:].rearrange("p j (m t) -> p m j t", t=PACK)[:, rows, :, first : first + 2],
             )
-            return woven
+
+        def woven_tile(name, first):
+            return new_tile([P, 2 * H], BF16, f"{name}_woven{first}")
 
         def quantize_w(woven, name, first):
             codes, scales = quantize(woven, 2 * P, name, first)
@@ -172,27 +177,31 @@ def tile_picked_hub_relu_e_kernel(tc, xT, w1, w2, w3_words, w3_scales, offs, src
 
         quantize_x(0, QUARTER)
         quantize_x(QUARTER, QUARTER)
-        w1_woven = [weave_w(nc.vector.tensor_copy, w1_raw, "w1", 0), weave_w(nc.scalar.copy, w1_raw, "w1", 2)]
+        w1_woven = [woven_tile("w1", 0), woven_tile("w1", 2)]
+        weave_w(nc.vector.tensor_copy, w1_raw, w1_woven[0], 0)
         w1_planes = quantize_w(w1_woven[0], "w1", 0)
         for piece in LATE_NODES:
             quantize_x(*piece)
+        weave_w(nc.vector.tensor_copy, w1_raw, w1_woven[1], 2, slice(0, P // 2))
+        weave_w(nc.scalar.copy, w1_raw, w1_woven[1], 2, slice(P // 2, P))
 
         y_all = new_tile([P, (PACK - 1) * S + WIDE], F32, "y_all")
         y = [y_all[:, (PACK - 1 - t) * S : (PACK - t) * S] for t in range(PACK)]
-        product(w1_planes[0], y[0], NODE_PIECES, (0, 1, 2, 3, 4), by_vector=(0, 2))
+        product(w1_planes[0], y[0], NODE_PIECES, (0, 1, 2, 3, 4), by_vector=(2,))
         w1_planes += quantize_w(w1_woven[1], "w1", 2)
-        product(w1_planes[1], y[1], HALVES, (2, 5))
-        w2_woven = [weave_w(nc.scalar.copy, w2_raw, "w2", 0)]
+        product(w1_planes[1], y[1], SECOND_PIECES, (5, 2, 3, 4))
+        w2_woven = [woven_tile("w2", 0), woven_tile("w2", 2)]
+        weave_w(nc.scalar.copy, w2_raw, w2_woven[0], 0)
         product(w1_planes[2], y[2], HALVES, (6, 7))
-        w2_woven.append(weave_w(nc.scalar.copy, w2_raw, "w2", 2))
+        weave_w(nc.scalar.copy, w2_raw, w2_woven[1], 2)
         product(w1_planes[3], y[3], HALVES, (0, 1))
 
         y_picked = []
-        sums = new_tile([P, PACK * UPPER_STEP], F32, "sums")
+        sums = new_tile([P, MIDDLE_AT + PACK * MIDDLE], F32, "sums")
 
         def gather_y(t):
-            if t == 2:
-                picked = sums[:, MIDDLE_AT - HALF : MIDDLE_AT + HALF]
+            if t == PACK - 1:
+                picked = sums[:, PICKED_AT : PICKED_AT + S]
             else:
                 picked = new_tile([P, S], F32, f"y_picked{t}")[:]
             start = (PACK - 1 - t) * S
@@ -206,10 +215,10 @@ def tile_picked_hub_relu_e_kernel(tc, xT, w1, w2, w3_words, w3_scales, offs, src
         w2_planes += quantize_w(w2_woven[1], "w2", 2)
         gather_y(3)
         e = [new_tile([P, S], F32, f"e{t}") for t in range(PACK)]
-        for t, where in ((0, (2, 3)), (1, (4, 5)), (3, (6, 7)), (2, (0, 1))):
-            product(w2_planes[t], e[t], HALVES, where)
+        for t in range(PACK):
+            product(w2_planes[t], e[t], HALVES, ((5, 2), (3, 4), (6, 7), (0, 1))[t])
 
-        upper = sums[:].rearrange("p (t n) -> p t n", t=PACK)[:, :, 0:HALF]
+        upper = sums[:, 0:PICKED_AT].rearrange("p (t n) -> p t n", t=PACK)
         middle = sums[:, MIDDLE_AT : MIDDLE_AT + PACK * MIDDLE].rearrange("p (t n) -> p t n", t=PACK)
         z = []
 
@@ -253,12 +262,10 @@ def tile_picked_hub_relu_e_kernel(tc, xT, w1, w2, w3_words, w3_scales, offs, src
             copy(out=result[:], in_=bank)
             nc.sync.dma_start(out=out[:, first : first + count], in_=result[:])
 
-        gather_e(0, HALF, HALF, upper[:, 0, :])
-        gather_e(1, HALF, HALF, upper[:, 1, :])
-        gather_e(3, LATE, S - LATE, sums[:, MIDDLE_AT + 3 * MIDDLE : 3 * UPPER_STEP + HALF])
-        gather_e(2, HALF, HALF, upper[:, 2, :])
+        for t in range(PACK):
+            gather_e(t, HALF, HALF, upper[:, t, :])
         relu(0, upper)
-        for t in (2, 0, 1):
+        for t in (3, 2, 1, 0):
             gather_e(t, LATE, MIDDLE, middle[:, t, :])
         relu(1, middle[:, :, LATE:MIDDLE])
         relu(2, middle[:, :, 0:LATE])

@@ -32,9 +32,9 @@ X_LOADS = (
 )
 ROW_ORDER = (0, 2, 1, 3)
 VECTOR_ENTRIES = (640, 640, 512, 512)
-NODE_PIECES = ((0, 256), (256, 256), (512, 256), (768, 128), (896, 128))
+NODE_PIECES = ((0, 256), (256, 256), (512, 128), (640, 128), (768, 128), (896, 128))
 SECOND_PIECES = ((768, 256), (512, 256), (0, 256), (256, 256))
-LATE_NODES = ((512, 256), (768, 256))
+LATE_NODES = NODE_PIECES[2:]
 QUARTER = 256
 WIDE = 1376
 EDGE_PIECES = ((512, 512), (256, 256), (128, 128), (0, 128))
@@ -49,7 +49,7 @@ AT = {
     "w1_woven0": 0,
     "x_codes1": 0,
     "w2_woven0": 2 * KIB,
-    "w1_codes0": 3 * KIB + KIB // 2,
+    "w1_codes1": 3 * KIB + 3 * KIB // 4,
     "w2_woven2": 4 * KIB,
     "x_picked": 6 * KIB,
     "w1_codes2": 6 * KIB,
@@ -141,7 +141,7 @@ def tile_picked_hub_relu_e_kernel(tc, xT, w1, w2, w3_words, w3_scales, offs, src
         def quantize(values, columns, name, index):
             codes = new_tile([P, columns], U32, f"{name}_codes{index}")
             scales = new_tile([P, columns], U8, f"{name}_scales{index}")
-            nc.vector.quantize_mx(out=codes[:].bitcast(FP8X4), scales=scales[:], in_=values[:])
+            nc.vector.quantize_mx(out=codes[:].bitcast(FP8X4), scales=scales[:], in_=values)
             return codes, scales
 
         def weave_w(copy, raw, woven, first, rows=slice(0, P)):
@@ -154,7 +154,7 @@ def tile_picked_hub_relu_e_kernel(tc, xT, w1, w2, w3_words, w3_scales, offs, src
             return new_tile([P, 2 * H], BF16, f"{name}_woven{first}")
 
         def quantize_w(woven, name, first):
-            codes, scales = quantize(woven, 2 * P, name, first)
+            codes, scales = quantize(woven[:], 2 * P, name, first)
             return [(codes[:, t * P : (t + 1) * P], scales[:, t * P : (t + 1) * P]) for t in range(2)]
 
         banks = [psum.tile([P, HALF], F32, name=f"bank{b}") for b in range(8)]
@@ -179,7 +179,10 @@ def tile_picked_hub_relu_e_kernel(tc, xT, w1, w2, w3_words, w3_scales, offs, src
         quantize_x(QUARTER, QUARTER)
         w1_woven = [woven_tile("w1", 0), woven_tile("w1", 2)]
         weave_w(nc.vector.tensor_copy, w1_raw, w1_woven[0], 0)
-        w1_planes = quantize_w(w1_woven[0], "w1", 0)
+        w1_planes = []
+        for t in range(2):
+            codes, scales = quantize(w1_woven[0][:, t * H : (t + 1) * H], P, "w1", t)
+            w1_planes.append((codes[:], scales[:]))
         for piece in LATE_NODES:
             quantize_x(*piece)
         weave_w(nc.vector.tensor_copy, w1_raw, w1_woven[1], 2, slice(0, P // 2))
@@ -187,14 +190,14 @@ def tile_picked_hub_relu_e_kernel(tc, xT, w1, w2, w3_words, w3_scales, offs, src
 
         y_all = new_tile([P, (PACK - 1) * S + WIDE], F32, "y_all")
         y = [y_all[:, (PACK - 1 - t) * S : (PACK - t) * S] for t in range(PACK)]
-        product(w1_planes[0], y[0], NODE_PIECES, (0, 1, 2, 3, 4), by_vector=(2,))
+        product(w1_planes[0], y[0], NODE_PIECES, (0, 1, 2, 3, 4, 5), by_vector=(3,))
         w1_planes += quantize_w(w1_woven[1], "w1", 2)
-        product(w1_planes[1], y[1], SECOND_PIECES, (5, 2, 3, 4))
+        product(w1_planes[1], y[1], SECOND_PIECES, (6, 3, 4, 5))
         w2_woven = [woven_tile("w2", 0), woven_tile("w2", 2)]
         weave_w(nc.scalar.copy, w2_raw, w2_woven[0], 0)
-        product(w1_planes[2], y[2], HALVES, (6, 7))
+        product(w1_planes[2], y[2], HALVES, (7, 0))
         weave_w(nc.scalar.copy, w2_raw, w2_woven[1], 2)
-        product(w1_planes[3], y[3], HALVES, (0, 1))
+        product(w1_planes[3], y[3], HALVES, (1, 2))
 
         y_picked = []
         sums = new_tile([P, MIDDLE_AT + PACK * MIDDLE], F32, "sums")
@@ -216,7 +219,7 @@ def tile_picked_hub_relu_e_kernel(tc, xT, w1, w2, w3_words, w3_scales, offs, src
         gather_y(3)
         e = [new_tile([P, S], F32, f"e{t}") for t in range(PACK)]
         for t in range(PACK):
-            product(w2_planes[t], e[t], HALVES, ((5, 2), (3, 4), (6, 7), (0, 1))[t])
+            product(w2_planes[t], e[t], HALVES, ((6, 3), (4, 5), (7, 0), (1, 2))[t])
 
         upper = sums[:, 0:PICKED_AT].rearrange("p (t n) -> p t n", t=PACK)
         middle = sums[:, MIDDLE_AT : MIDDLE_AT + PACK * MIDDLE].rearrange("p (t n) -> p t n", t=PACK)
@@ -235,7 +238,9 @@ def tile_picked_hub_relu_e_kernel(tc, xT, w1, w2, w3_words, w3_scales, offs, src
             z.append(new_tile([P, PACK * count], BF16, f"z{c}"))
             if c == LAST:
                 nc.vector.tensor_scalar_max(
-                    out=z[c][:].rearrange("p (n t) -> p n t", t=PACK), in0=values.rearrange("p t n -> p n t"), scalar1=0.0
+                    out=z[c][:].rearrange("p (g i t) -> p g t i", i=4, t=PACK),
+                    in0=values.rearrange("p t (g i) -> p g t i", i=4),
+                    scalar1=0.0,
                 )
             else:
                 nc.scalar.activation(
@@ -246,7 +251,7 @@ def tile_picked_hub_relu_e_kernel(tc, xT, w1, w2, w3_words, w3_scales, offs, src
 
         def finish(c):
             first, count = EDGE_PIECES[c]
-            codes, scales = quantize(z[c], count, "z", c)
+            codes, scales = quantize(z[c][:], count, "z", c)
             bank = banks[c][:, 0:count]
             nc.tensor.matmul_mx(
                 out=bank,

@@ -28,7 +28,7 @@ X_LOADS = (
     (1, 0, (0, 0, 1024)),
     (1, 1024, (0, 512, 512)),
     (3, 0, (0, 0, 1024)),
-    (3, 1024, (0, 512, 512)),
+    (3, 1024, (0, 576, 448)),
 )
 ROW_ORDER = (0, 2, 1, 3)
 VECTOR_ENTRIES = (640, 640, 512, 512)
@@ -36,6 +36,7 @@ NODE_PIECES = ((0, 256), (256, 256), (512, 128), (640, 128), (768, 128), (896, 1
 SECOND_PIECES = ((768, 256), (512, 256), (0, 256), (256, 256))
 LATE_NODES = NODE_PIECES[2:]
 QUARTER = 256
+VECTOR_ROWS = 48
 WIDE = 1376
 EDGE_PIECES = ((512, 512), (256, 256), (128, 128), (0, 128))
 LATE = 128
@@ -185,12 +186,12 @@ def tile_picked_hub_relu_e_kernel(tc, xT, w1, w2, w3_words, w3_scales, offs, src
             w1_planes.append((codes[:], scales[:]))
         for piece in LATE_NODES:
             quantize_x(*piece)
-        weave_w(nc.vector.tensor_copy, w1_raw, w1_woven[1], 2, slice(0, P // 2))
-        weave_w(nc.scalar.copy, w1_raw, w1_woven[1], 2, slice(P // 2, P))
+        weave_w(nc.vector.tensor_copy, w1_raw, w1_woven[1], 2, slice(0, VECTOR_ROWS))
+        weave_w(nc.scalar.copy, w1_raw, w1_woven[1], 2, slice(VECTOR_ROWS, P))
 
         y_all = new_tile([P, (PACK - 1) * S + WIDE], F32, "y_all")
         y = [y_all[:, (PACK - 1 - t) * S : (PACK - t) * S] for t in range(PACK)]
-        product(w1_planes[0], y[0], NODE_PIECES, (0, 1, 2, 3, 4, 5), by_vector=(3,))
+        product(w1_planes[0], y[0], NODE_PIECES, (0, 1, 2, 3, 4, 5), by_vector=(2, 3))
         w1_planes += quantize_w(w1_woven[1], "w1", 2)
         product(w1_planes[1], y[1], SECOND_PIECES, (6, 3, 4, 5))
         w2_woven = [woven_tile("w2", 0), woven_tile("w2", 2)]

@@ -22,21 +22,21 @@ HALF = 512
 HALVES = ((0, HALF), (HALF, HALF))
 
 X_LOADS = (
-    (0, 0, (1408, 640, 0)),
-    (2, 0, (0, 0, 1024)),
-    (2, 1024, (0, 512, 512)),
+    (2, 0, (1024, 0, 0)),
+    (2, 1024, (768, 256, 0)),
+    (0, 0, (0, 0, 1024)),
+    (0, 1024, (0, 512, 512)),
     (1, 0, (0, 0, 1024)),
     (1, 1024, (0, 512, 512)),
     (3, 0, (0, 0, 1024)),
-    (3, 1024, (0, 576, 448)),
+    (3, 1024, (0, 512, 512)),
 )
-ROW_ORDER = (0, 2, 1, 3)
+ROW_ORDER = (2, 0, 1, 3)
 VECTOR_ENTRIES = (640, 640, 512, 512)
 NODE_PIECES = ((0, 256), (256, 256), (512, 128), (640, 128), (768, 128), (896, 128))
 SECOND_PIECES = ((768, 256), (512, 256), (0, 256), (256, 256))
 LATE_NODES = NODE_PIECES[2:]
 QUARTER = 256
-VECTOR_ROWS = 48
 WIDE = 1376
 EDGE_PIECES = ((512, 512), (256, 256), (128, 128), (0, 128))
 LATE = 128
@@ -145,10 +145,10 @@ def tile_picked_hub_relu_e_kernel(tc, xT, w1, w2, w3_words, w3_scales, offs, src
             nc.vector.quantize_mx(out=codes[:].bitcast(FP8X4), scales=scales[:], in_=values)
             return codes, scales
 
-        def weave_w(copy, raw, woven, first, rows=slice(0, P)):
+        def weave_w(copy, raw, woven, first):
             copy(
-                out=woven[:].rearrange("p (t m j) -> p m j t", t=2, j=PACK)[:, rows],
-                in_=raw[:].rearrange("p j (m t) -> p m j t", t=PACK)[:, rows, :, first : first + 2],
+                out=woven[:].rearrange("p (t m j) -> p m j t", t=2, j=PACK),
+                in_=raw[:].rearrange("p j (m t) -> p m j t", t=PACK)[:, :, :, first : first + 2],
             )
 
         def woven_tile(name, first):
@@ -186,8 +186,7 @@ def tile_picked_hub_relu_e_kernel(tc, xT, w1, w2, w3_words, w3_scales, offs, src
             w1_planes.append((codes[:], scales[:]))
         for piece in LATE_NODES:
             quantize_x(*piece)
-        weave_w(nc.vector.tensor_copy, w1_raw, w1_woven[1], 2, slice(0, VECTOR_ROWS))
-        weave_w(nc.scalar.copy, w1_raw, w1_woven[1], 2, slice(VECTOR_ROWS, P))
+        weave_w(nc.scalar.copy, w1_raw, w1_woven[1], 2)
 
         y_all = new_tile([P, (PACK - 1) * S + WIDE], F32, "y_all")
         y = [y_all[:, (PACK - 1 - t) * S : (PACK - t) * S] for t in range(PACK)]

@@ -190,7 +190,7 @@ def tile_picked_hub_relu_e_kernel(tc, xT, w1, w2, w3_words, w3_scales, offs, src
 
         y_all = new_tile([P, (PACK - 1) * S + WIDE], F32, "y_all")
         y = [y_all[:, (PACK - 1 - t) * S : (PACK - t) * S] for t in range(PACK)]
-        product(w1_planes[0], y[0], NODE_PIECES, (0, 1, 2, 3, 4, 5), by_vector=(2, 3))
+        product(w1_planes[0], y[0], NODE_PIECES, (0, 1, 2, 3, 4, 5), by_vector=(1, 3))
         w1_planes += quantize_w(w1_woven[1], "w1", 2)
         product(w1_planes[1], y[1], SECOND_PIECES, (6, 3, 4, 5))
         w2_woven = [woven_tile("w2", 0), woven_tile("w2", 2)]

@@ -34,26 +34,17 @@ X_LOADS = (
 ROW_ORDER = (2, 0, 1, 3)
 VECTOR_ENTRIES = (640, 640, 512, 512)
 NODE_PIECES = ((0, 256), (256, 256), (512, 128), (640, 128), (768, 128), (896, 128))
-SECOND_PIECES = ((768, 256), (512, 256), (0, 256), (256, 256))
 LATE_NODES = NODE_PIECES[2:]
 QUARTER = 256
-WIDE = 1376
-EDGE_PIECES = ((512, 512), (256, 256), (128, 128), (0, 128))
-LATE = 128
-MIDDLE = HALF - LATE
-PICKED_AT = PACK * HALF
-MIDDLE_AT = PICKED_AT + HALF + (HALF - MIDDLE) // 2 - MIDDLE
-LAST = len(EDGE_PIECES) - 1
+SPARE = 16
+EDGE_PIECES = ((0, 256), (256, 256), (512, 128), (640, 128), (768, 128), (896, 128))
+LAST_GATHERS = ((0, 256), (256, 256), (512, 256), (768, 256))
 
 KIB = 1024
 AT = {
     "w1_woven0": 0,
     "x_codes1": 0,
-    "w2_woven0": 2 * KIB,
-    "w1_codes1": 3 * KIB + 3 * KIB // 4,
-    "w2_woven2": 4 * KIB,
     "x_picked": 6 * KIB,
-    "w1_codes2": 6 * KIB,
 }
 
 
@@ -88,14 +79,13 @@ def tile_picked_hub_relu_e_kernel(tc, xT, w1, w2, w3_words, w3_scales, offs, src
             if i == 0:
                 nc.sync.dma_start(offs_sb[:], offs)
 
-        def load_w(w, name):
-            raw = new_tile([P, PACK, H], F32, name)
-            nc.sync.dma_start(out=raw[:], in_=w.rearrange("(p j) c -> p j c", j=PACK))
+        def load_w(w, raw):
+            nc.sync.dma_start(out=raw, in_=w.rearrange("(p j) c -> p (j c)", j=PACK))
             return raw
 
-        w1_raw = load_w(w1, "w1_raw")
+        w1_raw = load_w(w1, new_tile([P, PACK * H], F32, "w1_raw")[:])
         nc.sync.dma_start(src_sb[:], src)
-        w2_raw = load_w(w2, "w2_raw")
+        w2_raw = load_w(w2, new_tile([P, PACK * H], F32, "w2_raw")[:])
         nc.sync.dma_start(dst_sb[:], dst)
         nc.sync.dma_start(out=w3_codes[:].bitcast(I32), in_=w3_words[0].bitcast(I32))
         for q in range(4):
@@ -147,16 +137,16 @@ def tile_picked_hub_relu_e_kernel(tc, xT, w1, w2, w3_words, w3_scales, offs, src
 
         def weave_w(copy, raw, woven, first):
             copy(
-                out=woven[:].rearrange("p (t m j) -> p m j t", t=2, j=PACK),
-                in_=raw[:].rearrange("p j (m t) -> p m j t", t=PACK)[:, :, :, first : first + 2],
+                out=woven.rearrange("p (t m j) -> p m j t", t=2, j=PACK),
+                in_=raw.rearrange("p (j m t) -> p m j t", j=PACK, t=PACK)[:, :, :, first : first + 2],
             )
 
         def woven_tile(name, first):
             return new_tile([P, 2 * H], BF16, f"{name}_woven{first}")
 
-        def quantize_w(woven, name, first):
-            codes, scales = quantize(woven[:], 2 * P, name, first)
-            return [(codes[:, t * P : (t + 1) * P], scales[:, t * P : (t + 1) * P]) for t in range(2)]
+        def quantize_w(woven, planes, name):
+            codes, scales = quantize(woven, planes * P, name, 0)
+            return [(codes[:, t * P : (t + 1) * P], scales[:, t * P : (t + 1) * P]) for t in range(planes)]
 
         banks = [psum.tile([P, HALF], F32, name=f"bank{b}") for b in range(8)]
 
@@ -178,107 +168,110 @@ def tile_picked_hub_relu_e_kernel(tc, xT, w1, w2, w3_words, w3_scales, offs, src
 
         quantize_x(0, QUARTER)
         quantize_x(QUARTER, QUARTER)
-        w1_woven = [woven_tile("w1", 0), woven_tile("w1", 2)]
-        weave_w(nc.vector.tensor_copy, w1_raw, w1_woven[0], 0)
+        w1_woven = woven_tile("w1", 0)
+        weave_w(nc.vector.tensor_copy, w1_raw, w1_woven[:], 0)
         w1_planes = []
         for t in range(2):
-            codes, scales = quantize(w1_woven[0][:, t * H : (t + 1) * H], P, "w1", t)
+            codes, scales = quantize(w1_woven[:, t * H : (t + 1) * H], P, "w1", t)
             w1_planes.append((codes[:], scales[:]))
         for piece in LATE_NODES:
             quantize_x(*piece)
-        weave_w(nc.scalar.copy, w1_raw, w1_woven[1], 2)
+        late_woven = new_tile([P, PACK * H], BF16, "late_woven")[:]
+        weave_w(nc.scalar.copy, w1_raw, late_woven[:, 0 : 2 * H], 2)
 
-        y_all = new_tile([P, (PACK - 1) * S + WIDE], F32, "y_all")
-        y = [y_all[:, (PACK - 1 - t) * S : (PACK - t) * S] for t in range(PACK)]
-        product(w1_planes[0], y[0], NODE_PIECES, (0, 1, 2, 3, 4, 5), by_vector=(1, 3))
-        w1_planes += quantize_w(w1_woven[1], "w1", 2)
-        product(w1_planes[1], y[1], SECOND_PIECES, (6, 3, 4, 5))
-        w2_woven = [woven_tile("w2", 0), woven_tile("w2", 2)]
-        weave_w(nc.scalar.copy, w2_raw, w2_woven[0], 0)
-        product(w1_planes[2], y[2], HALVES, (7, 0))
-        weave_w(nc.scalar.copy, w2_raw, w2_woven[1], 2)
-        product(w1_planes[3], y[3], HALVES, (1, 2))
+        y = [new_tile([P, S + SPARE], F32, f"y{t}") for t in range(PACK)]
+        e = [new_tile([P, S + SPARE], F32, f"e{t}") for t in range(PACK)]
+        y_picked = [new_tile([P, S], F32, f"y_picked{t}") for t in range(PACK)]
+        sums = new_tile([P, PACK, S], F32, "sums")
 
-        y_picked = []
-        sums = new_tile([P, MIDDLE_AT + PACK * MIDDLE], F32, "sums")
+        def gather_y(t, first, count):
+            nc.scalar.activation(
+                out=y_picked[t][:, first : first + count], in_=y[t][:].indirect(entries(src_sb, first, count)), func=ACT.Copy
+            )
 
-        def gather_y(t):
-            if t == PACK - 1:
-                picked = sums[:, PICKED_AT : PICKED_AT + S]
-            else:
-                picked = new_tile([P, S], F32, f"y_picked{t}")[:]
-            start = (PACK - 1 - t) * S
-            nc.vector.tensor_copy(out=picked, in_=y_all[:, start : start + WIDE].indirect(src_sb[:]))
-            y_picked.append(picked)
-
-        gather_y(0)
-        gather_y(1)
-        w2_planes = quantize_w(w2_woven[0], "w2", 0)
-        gather_y(2)
-        w2_planes += quantize_w(w2_woven[1], "w2", 2)
-        gather_y(3)
-        e = [new_tile([P, S], F32, f"e{t}") for t in range(PACK)]
-        for t in range(PACK):
-            product(w2_planes[t], e[t], HALVES, ((6, 3), (4, 5), (7, 0), (1, 2))[t])
-
-        upper = sums[:, 0:PICKED_AT].rearrange("p (t n) -> p t n", t=PACK)
-        middle = sums[:, MIDDLE_AT : MIDDLE_AT + PACK * MIDDLE].rearrange("p (t n) -> p t n", t=PACK)
-        z = []
-
-        def gather_e(t, first, count, target):
+        def gather_e(t, first, count):
             nc.vector.tensor_tensor(
-                out=target,
+                out=sums[:, t, first : first + count],
                 in0=e[t][:].indirect(entries(dst_sb, first, count)),
                 in1=y_picked[t][:, first : first + count],
                 op=ADD,
             )
 
-        def relu(c, values):
+        z = {}
+        result = new_tile([P, S], F32, "result")
+
+        def relu(c, on_vector):
             first, count = EDGE_PIECES[c]
-            z.append(new_tile([P, PACK * count], BF16, f"z{c}"))
-            if c == LAST:
-                nc.vector.tensor_scalar_max(
-                    out=z[c][:].rearrange("p (g i t) -> p g t i", i=4, t=PACK),
-                    in0=values.rearrange("p t (g i) -> p g t i", i=4),
-                    scalar1=0.0,
-                )
+            z[c] = new_tile([P, PACK * count], BF16, f"z{c}")[:]
+            woven = z[c].rearrange("p (g i t) -> p g t i", i=4, t=PACK)
+            values = sums[:, :, first : first + count].rearrange("p t (g i) -> p g t i", i=4)
+            if on_vector:
+                nc.vector.tensor_scalar_max(out=woven, in0=values, scalar1=0.0)
             else:
-                nc.scalar.activation(
-                    out=z[c][:].rearrange("p (g i t) -> p g t i", i=4, t=PACK),
-                    in_=values.rearrange("p t (g i) -> p g t i", i=4),
-                    func=ACT.Relu,
-                )
+                nc.scalar.activation(out=woven, in_=values, func=ACT.Relu)
 
-        def finish(c):
+        def finish(c, b, copy):
             first, count = EDGE_PIECES[c]
-            codes, scales = quantize(z[c][:], count, "z", c)
-            bank = banks[c][:, 0:count]
-            nc.tensor.matmul_mx(
-                out=bank,
-                lhsT=w3_codes[:].bitcast(FP4X4),
-                lhsT_scale=w3_bytes[:],
-                rhs=codes[:].bitcast(FP8X4),
-                rhs_scale=scales[:],
-                start=True,
-                stop=True,
-            )
-            result = new_tile([P, count], F32, f"result{c}")
-            copy = nc.vector.tensor_copy if c == LAST else nc.scalar.copy
-            copy(out=result[:], in_=bank)
-            nc.sync.dma_start(out=out[:, first : first + count], in_=result[:])
+            codes, scales = quantize(z[c], count, "z", c)
+            for start in range(0, count, QUARTER):
+                columns = slice(start, min(start + QUARTER, count))
+                nc.tensor.matmul_mx(
+                    out=banks[b][:, columns],
+                    lhsT=w3_codes[:].bitcast(FP4X4),
+                    lhsT_scale=w3_bytes[:],
+                    rhs=codes[:, columns].bitcast(FP8X4),
+                    rhs_scale=scales[:, columns],
+                    start=True,
+                    stop=True,
+                )
+            copy(out=result[:, first : first + count], in_=banks[b][:, 0:count])
 
-        for t in range(PACK):
-            gather_e(t, HALF, HALF, upper[:, t, :])
-        relu(0, upper)
-        for t in (3, 2, 1, 0):
-            gather_e(t, LATE, MIDDLE, middle[:, t, :])
-        relu(1, middle[:, :, LATE:MIDDLE])
-        relu(2, middle[:, :, 0:LATE])
-        finish(0)
-        late = upper[:, :, 0:LATE]
-        for t in range(PACK):
-            gather_e(t, 0, LATE, late[:, t, :])
-        finish(1)
-        relu(LAST, late)
-        finish(2)
-        finish(LAST)
+        def store(view):
+            nc.sync.dma_start(out=view(out), in_=view(result[:]))
+
+        both = (0, 1)
+        product(w1_planes[0], y[0], NODE_PIECES, (0, 1, 2, 3, 4, 5), by_vector=(1,))
+        gather_y(0, 0, S)
+        w2_woven = woven_tile("w2", 0)
+        weave_w(nc.vector.tensor_copy, w2_raw, w2_woven[:], 0)
+        w2_planes = quantize_w(w2_woven[:], 2, "w2")
+        weave_w(nc.vector.tensor_copy, w2_raw, late_woven[:, 2 * H : PACK * H], 2)
+        late_planes = quantize_w(late_woven, PACK, "late_w")
+        w1_planes += late_planes[0:2]
+        w2_planes += late_planes[2:PACK]
+        product(w1_planes[1], y[1], HALVES[0:1], (4,))
+        product(w2_planes[0], e[0], HALVES, (6, 7), by_vector=both)
+        product(w1_planes[1], y[1], HALVES[1:2], (6,))
+        gather_y(1, 0, S)
+        gather_e(0, 0, S)
+        product(w2_planes[1], e[1], HALVES, (0, 1), by_vector=both)
+        product(w1_planes[2], y[2], HALVES, (2, 7))
+        gather_y(2, 0, S)
+        product(w2_planes[2], e[2], HALVES, (5, 3), by_vector=both)
+        product(w2_planes[3], e[3], ((0, 256),), (0,), by_vector=(0,))
+        gather_e(1, 0, S)
+        gather_e(2, 0, S)
+        product(w1_planes[3], y[3], HALVES, (7, 1))
+        product(w2_planes[3], e[3], ((256, 256), (512, 512)), (5, 3))
+        for piece in LAST_GATHERS:
+            gather_y(3, *piece)
+        gather_e(3, *LAST_GATHERS[0])
+        gather_e(3, *LAST_GATHERS[1])
+        relu(0, True)
+        relu(1, False)
+        gather_e(3, *LAST_GATHERS[2])
+        finish(0, 0, nc.scalar.copy)
+        store(lambda ap: ap[:, 0:256])
+        relu(2, False)
+        relu(3, False)
+        gather_e(3, *LAST_GATHERS[3])
+        finish(1, 2, nc.scalar.copy)
+        store(lambda ap: ap[:, 256:512])
+        relu(4, True)
+        finish(2, 4, nc.scalar.copy)
+        relu(5, True)
+        finish(4, 6, nc.scalar.copy)
+        store(lambda ap: ap.rearrange("p (h n) -> p h n", h=4)[:, 2:4, 0:128])
+        finish(3, 7, nc.vector.tensor_copy)
+        finish(5, 1, nc.vector.tensor_copy)
+        store(lambda ap: ap.rearrange("p (h n) -> p h n", h=4)[:, 2:4, 128:256])

@@ -248,11 +248,10 @@ def tile_picked_hub_relu_e_kernel(tc, xT, w1, w2, w3_words, w3_scales, offs, src
         product(w1_planes[2], y[2], HALVES, (2, 7))
         gather_y(2, 0, S)
         product(w2_planes[2], e[2], HALVES, (5, 3), by_vector=both)
-        product(w2_planes[3], e[3], ((0, 256),), (0,), by_vector=(0,))
         gather_e(1, 0, S)
         gather_e(2, 0, S)
         product(w1_planes[3], y[3], HALVES, (7, 1))
-        product(w2_planes[3], e[3], ((256, 256), (512, 512)), (5, 3))
+        product(w2_planes[3], e[3], HALVES, (5, 3))
         for piece in LAST_GATHERS:
             gather_y(3, *piece)
         gather_e(3, *LAST_GATHERS[0])
@@ -260,18 +259,18 @@ def tile_picked_hub_relu_e_kernel(tc, xT, w1, w2, w3_words, w3_scales, offs, src
         relu(0, True)
         relu(1, False)
         gather_e(3, *LAST_GATHERS[2])
-        finish(0, 0, nc.scalar.copy)
-        store(lambda ap: ap[:, 0:256])
         relu(2, False)
         relu(3, False)
         gather_e(3, *LAST_GATHERS[3])
+        finish(0, 0, nc.scalar.copy)
+        store(lambda ap: ap[:, 0:256])
+        relu(4, True)
         finish(1, 2, nc.scalar.copy)
         store(lambda ap: ap[:, 256:512])
-        relu(4, True)
-        finish(2, 4, nc.scalar.copy)
         relu(5, True)
         finish(4, 6, nc.scalar.copy)
+        finish(2, 4, nc.scalar.copy)
         store(lambda ap: ap.rearrange("p (h n) -> p h n", h=4)[:, 2:4, 0:128])
-        finish(3, 7, nc.vector.tensor_copy)
         finish(5, 1, nc.vector.tensor_copy)
+        finish(3, 7, nc.vector.tensor_copy)
         store(lambda ap: ap.rearrange("p (h n) -> p h n", h=4)[:, 2:4, 128:256])

from contextlib import ExitStack

import concourse.mybir as mybir

K, T, S, H, N = 512, 2048, 1024, 512, 128
FLOPS = 2 * K * H * S * 2 + 2 * H * N * S

F32 = mybir.dt.float32
BF16 = mybir.dt.bfloat16
I32 = mybir.dt.int32
U32 = mybir.dt.uint32
U16 = mybir.dt.uint16
U8 = mybir.dt.uint8
FP8X4 = mybir.dt.float8_e4m3fn_x4
FP4X4 = mybir.dt.float4_e2m1fn_x4
ACT = mybir.ActivationFunctionType
ADD = mybir.AluOpType.add

P = 128
PACK = 4
HALF = 512
HALVES = ((0, HALF), (HALF, HALF))

X_LOADS = (
    (2, 0, (1024, 0, 0)),
    (2, 1024, (768, 256, 0)),
    (0, 0, (0, 0, 1024)),
    (0, 1024, (0, 512, 512)),
    (1, 0, (0, 0, 1024)),
    (1, 1024, (0, 512, 512)),
    (3, 0, (0, 0, 1024)),
    (3, 1024, (0, 512, 512)),
)
ROW_ORDER = (2, 0, 1, 3)
VECTOR_ENTRIES = (640, 640, 512, 512)
NODE_PIECES = ((0, 256), (256, 256), (512, 128), (640, 128), (768, 128), (896, 128))
LATE_NODES = NODE_PIECES[2:]
QUARTER = 256
SPARE = 16
EDGE_PIECES = ((0, 256), (256, 256), (512, 128), (640, 128), (768, 128), (896, 128))
LAST_GATHERS = ((0, 256), (256, 256), (512, 256), (768, 256))

KIB = 1024
AT = {
    "w1_woven0": 0,
    "x_codes1": 0,
    "x_picked": 6 * KIB,
}


def tile_picked_hub_relu_e_kernel(tc, xT, w1, w2, w3_words, w3_scales, offs, src, dst, out):
    nc = tc.nc
    with ExitStack() as ctx:
        keep = ctx.enter_context(tc.tile_pool(name="keep", bufs=1))
        shared = ctx.enter_context(tc.tile_pool(name="shared", bufs=1))
        psum = ctx.enter_context(tc.psum_pool(name="psum", bufs=1))

        def new_tile(shape, dtype, name):
            if name in AT:
                return shared.tile(shape, dtype, name=name, align_bytes=64, offset=AT[name])
            return keep.tile(shape, dtype, name=name, align_bytes=64)

        offs_sb = keep.tile([P, S // 16], U16, name="offs_sb")
        dst_sb = keep.tile([P, S // 16], U16, name="dst_sb")
        src_sb = keep.tile([P, S // 16], U16, name="src_sb")

        def entries(lst, first, count):
            return lst[:, first // 16 : (first + count) // 16]

        w3_bytes = new_tile([P, N], U8, "w3_bytes")
        w3_codes = new_tile([P, 2 * N], U8, "w3_codes")
        nc.vector.memset(w3_bytes[:].bitcast(I32), 0)

        x_rows = xT.rearrange("(p j) t -> p j t", j=PACK)
        x_raw = [new_tile([P, T], F32, f"x_raw{j}") for j in range(PACK)]
        for i, (j, first, shares) in enumerate(X_LOADS):
            nodes = slice(first, first + sum(shares))
            nc.sync.dma_start(out=x_raw[j][:, nodes], in_=x_rows[:, j, nodes])
            if i == 0:
                nc.sync.dma_start(offs_sb[:], offs)

        def load_w(w, raw):
            nc.sync.dma_start(out=raw, in_=w.rearrange("(p j) c -> p (j c)", j=PACK))
            return raw

        w1_raw = load_w(w1, new_tile([P, PACK * H], F32, "w1_raw")[:])
        nc.sync.dma_start(src_sb[:], src)
        w2_raw = load_w(w2, new_tile([P, PACK * H], F32, "w2_raw")[:])
        nc.sync.dma_start(dst_sb[:], dst)
        nc.sync.dma_start(out=w3_codes[:].bitcast(I32), in_=w3_words[0].bitcast(I32))
        for q in range(4):
            nc.sync.dma_start(
                out=w3_bytes[32 * q : 32 * q + 4, :].bitcast(I32),
                in_=w3_scales[0, 4 * q : 4 * q + 4, :].bitcast(I32),
            )

        x_rounded = [new_tile([P, T], BF16, f"x_rounded{j}") for j in range(PACK)]
        x_picked = new_tile([P, PACK * S], BF16, "x_picked")
        picked_rows = x_picked[:].rearrange("p (n j) -> p n j", j=PACK)
        for j in ROW_ORDER:
            for row, first, shares in X_LOADS:
                if row == j:
                    for count, copy in zip(shares, (nc.vector.tensor_copy, nc.scalar.copy, nc.gpsimd.tensor_copy)):
                        if count:
                            copy(out=x_rounded[j][:, first : first + count], in_=x_raw[j][:, first : first + count])
                        first = first + count
            split = VECTOR_ENTRIES[j]
            step = QUARTER if j == PACK - 1 else split
            for first in range(0, split, step):
                nc.vector.tensor_copy(
                    out=picked_rows[:, first : first + step, j], in_=x_raw[j][:].indirect(entries(offs_sb, first, step))
                )
            nc.scalar.activation(
                out=picked_rows[:, split:S, j], in_=x_rounded[j][:].indirect(entries(offs_sb, split, S - split)), func=ACT.Copy
            )

        x_codes = []
        x_scales = new_tile([P, S], U8, "x_scales")

        def x_words(first, count):
            return x_codes[first // HALF][:, first % HALF : first % HALF + count].bitcast(FP8X4)

        def quantize_x(first, count):
            if first % HALF == 0:
                x_codes.append(new_tile([P, HALF], U32, f"x_codes{first // HALF}"))
            nc.vector.quantize_mx(
                out=x_words(first, count),
                scales=x_scales[:, first : first + count],
                in_=x_picked[:, PACK * first : PACK * (first + count)],
            )

        def quantize(values, columns, name, index):
            codes = new_tile([P, columns], U32, f"{name}_codes{index}")
            scales = new_tile([P, columns], U8, f"{name}_scales{index}")
            nc.vector.quantize_mx(out=codes[:].bitcast(FP8X4), scales=scales[:], in_=values)
            return codes, scales

        def weave_w(copy, raw, woven, first):
            copy(
                out=woven.rearrange("p (t m j) -> p m j t", t=2, j=PACK),
                in_=raw.rearrange("p (j m t) -> p m j t", j=PACK, t=PACK)[:, :, :, first : first + 2],
            )

        def woven_tile(name, first):
            return new_tile([P, 2 * H], BF16, f"{name}_woven{first}")

        def quantize_w(woven, planes, name):
            codes, scales = quantize(woven, planes * P, name, 0)
            return [(codes[:, t * P : (t + 1) * P], scales[:, t * P : (t + 1) * P]) for t in range(planes)]

        banks = [psum.tile([P, HALF], F32, name=f"bank{b}") for b in range(8)]

        def product(weights, plane, pieces, where, by_vector=()):
            codes, scales = weights
            for i, (first, count) in enumerate(pieces):
                bank = banks[where[i]][:, 0:count]
                nc.tensor.matmul_mx(
                    out=bank,
                    lhsT=codes.bitcast(FP8X4),
                    lhsT_scale=scales,
                    rhs=x_words(first, count),
                    rhs_scale=x_scales[:, first : first + count],
                    start=True,
                    stop=True,
                )
                copy = nc.vector.tensor_copy if i in by_vector else nc.scalar.copy
                copy(out=plane[:, first : first + count], in_=bank)

        quantize_x(0, QUARTER)
        quantize_x(QUARTER, QUARTER)
        w1_woven = woven_tile("w1", 0)
        weave_w(nc.vector.tensor_copy, w1_raw, w1_woven[:], 0)
        w1_planes = []
        for t in range(2):
            codes, scales = quantize(w1_woven[:, t * H : (t + 1) * H], P, "w1", t)
            w1_planes.append((codes[:], scales[:]))
        for piece in LATE_NODES:
            quantize_x(*piece)
        late_woven = new_tile([P, PACK * H], BF16, "late_woven")[:]
        weave_w(nc.scalar.copy, w1_raw, late_woven[:, 0 : 2 * H], 2)

        y = [new_tile([P, S + SPARE], F32, f"y{t}") for t in range(PACK)]
        e = [new_tile([P, S + SPARE], F32, f"e{t}") for t in range(PACK)]
        y_picked = [new_tile([P, S], F32, f"y_picked{t}") for t in range(PACK)]
        sums = new_tile([P, PACK, S], F32, "sums")

        def gather_y(t, first, count):
            nc.scalar.activation(
                out=y_picked[t][:, first : first + count], in_=y[t][:].indirect(entries(src_sb, first, count)), func=ACT.Copy
            )

        def gather_e(t, first, count):
            nc.vector.tensor_tensor(
                out=sums[:, t, first : first + count],
                in0=e[t][:].indirect(entries(dst_sb, first, count)),
                in1=y_picked[t][:, first : first + count],
                op=ADD,
            )

        z = {}
        result = new_tile([P, S], F32, "result")

        def relu(c, on_vector):
            first, count = EDGE_PIECES[c]
            z[c] = new_tile([P, PACK * count], BF16, f"z{c}")[:]
            woven = z[c].rearrange("p (g i t) -> p g t i", i=4, t=PACK)
            values = sums[:, :, first : first + count].rearrange("p t (g i) -> p g t i", i=4)
            if on_vector:
                nc.vector.tensor_scalar_max(out=woven, in0=values, scalar1=0.0)
            else:
                nc.scalar.activation(out=woven, in_=values, func=ACT.Relu)

        def finish(c, b, copy):
            first, count = EDGE_PIECES[c]
            codes, scales = quantize(z[c], count, "z", c)
            for start in range(0, count, QUARTER):
                columns = slice(start, min(start + QUARTER, count))
                nc.tensor.matmul_mx(
                    out=banks[b][:, columns],
                    lhsT=w3_codes[:].bitcast(FP4X4),
                    lhsT_scale=w3_bytes[:],
                    rhs=codes[:, columns].bitcast(FP8X4),
                    rhs_scale=scales[:, columns],
                    start=True,
                    stop=True,
                )
            copy(out=result[:, first : first + count], in_=banks[b][:, 0:count])

        def store(view):
            nc.sync.dma_start(out=view(out), in_=view(result[:]))

        both = (0, 1)
        product(w1_planes[0], y[0], NODE_PIECES, (0, 1, 2, 3, 4, 5), by_vector=(1,))
        gather_y(0, 0, S)
        w2_woven = woven_tile("w2", 0)
        weave_w(nc.vector.tensor_copy, w2_raw, w2_woven[:], 0)
        w2_planes = quantize_w(w2_woven[:], 2, "w2")
        weave_w(nc.vector.tensor_copy, w2_raw, late_woven[:, 2 * H : PACK * H], 2)
        late_planes = quantize_w(late_woven, PACK, "late_w")
        w1_planes += late_planes[0:2]
        w2_planes += late_planes[2:PACK]
        product(w1_planes[1], y[1], HALVES[0:1], (4,))
        product(w2_planes[0], e[0], HALVES, (6, 7), by_vector=both)
        product(w1_planes[1], y[1], HALVES[1:2], (6,))
        gather_y(1, 0, S)
        gather_e(0, 0, S)
        product(w2_planes[1], e[1], HALVES, (0, 1), by_vector=both)
        product(w1_planes[2], y[2], HALVES, (2, 7))
        gather_y(2, 0, S)
        product(w2_planes[2], e[2], HALVES, (5, 3), by_vector=both)
        gather_e(1, 0, S)
        gather_e(2, 0, S)
        product(w1_planes[3], y[3], HALVES, (7, 1))
        product(w2_planes[3], e[3], HALVES, (5, 3))
        for piece in LAST_GATHERS:
            gather_y(3, *piece)
        gather_e(3, *LAST_GATHERS[0])
        gather_e(3, *LAST_GATHERS[1])
        relu(0, True)
        relu(1, False)
        gather_e(3, *LAST_GATHERS[2])
        relu(2, False)
        relu(3, False)
        gather_e(3, *LAST_GATHERS[3])
        finish(0, 0, nc.scalar.copy)
        store(lambda ap: ap[:, 0:256])
        relu(4, True)
        finish(1, 2, nc.scalar.copy)
        store(lambda ap: ap[:, 256:512])
        relu(5, True)
        finish(4, 6, nc.scalar.copy)
        finish(2, 4, nc.scalar.copy)
        store(lambda ap: ap.rearrange("p (h n) -> p h n", h=4)[:, 2:4, 0:128])
        finish(5, 1, nc.vector.tensor_copy)
        finish(3, 7, nc.vector.tensor_copy)
        store(lambda ap: ap.rearrange("p (h n) -> p h n", h=4)[:, 2:4, 128:256])
